import numpy as np, ml_dtypes
CORES = [1,5,17,21,33,37,49,53]
N = 8
BF = ml_dtypes.bfloat16
def gentries(a):
    return np.ascontiguousarray(a.reshape(8, 16, -1).transpose(0, 2, 1)).reshape(8, -1)
def gtable(e):
    e = np.asarray(e); return np.ascontiguousarray(e.reshape(8, -1, 16).transpose(0, 2, 1)).reshape(128, -1).astype(np.int32)
W, C, T, S = 4096, 192, 3, 3
K = 16 * C; H = 8 * C
EX = np.exp(-0.015625 * np.arange(256))
def pack(Y, R, L, D, F):
    return {"wl": np.ascontiguousarray(Y.reshape(N, 128, W)).astype(np.float32).astype(BF), "rc": np.ascontiguousarray(R.reshape(N, 128, K)).astype(np.float32).astype(BF),
            "nm": np.stack([gtable(a) for a in L]), "dn": np.ascontiguousarray(D).astype(np.int32), "pl": np.ascontiguousarray(F).astype(np.int32)}
def names(rng):
    return np.ascontiguousarray(np.argsort(rng.random((N, 8, 2, W)), axis=-1)[..., :H]).reshape(N, 8, K)
def flows(rng):
    return np.argsort(rng.random((N, 8, W)), axis=-1)
def records(rng, k):
    v = rng.integers(0, 256, (N, 8, 16, k)); v[:, :, :15] = v[:, :, :15] >> rng.integers(0, 2, (N, 8, 1, k)); v[:, :, 15] = rng.integers(0, 160, (N, 8, k))
    return v * (rng.random((N, 8, 1, k)) > 0.125)
def thin(rng, R):
    share = rng.choice(np.array([0.0, 0.0, 0.25, 0.5]), (N, 8, 1, C, 1))
    return (R.reshape(N, 8, 16, C, 16) * (rng.random((N, 8, 1, C, 16)) >= share)).reshape(N, 8, 16, K)
def steady(rng, size, lo, hi):
    v = np.zeros((N, 8, 16, K), np.int64); v[:, :, :15] = size * (1 + np.argsort(rng.random((N, 8, 15, K)), axis=2)); v[:, :, 15] = rng.integers(lo, hi, (N, 8, K))
    return v
def alive(rng, m):
    return (np.argsort(rng.random((N, 8, C, 16)), axis=3) < m[..., None]).reshape(N, 8, 1, K)
def lanes(a):
    return np.repeat(a, 16, axis=2)[:, :, None, :]
def mixed(rng, k):
    v = 255 * rng.integers(0, 2, (N, 8, 16, k)); t = rng.integers(0, 5, (N, 8, 1, k))
    v = np.where(t == 0, 0, np.where((t == 1) | (t == 2), 255, v)); t = t[:, :, 0]
    v[:, :, 15] = np.where(t == 2, 0, np.where(t == 4, 255, v[:, :, 15]))
    return v
def strong(rng):
    a = rng.integers(130, 231, (N, 8, C)); c = np.repeat(a, 16, axis=2) + (rng.random((N, 8, K)) < 0.25).astype(np.int64)
    b = (16 * c + rng.integers(0, 9, (N, 8, K)))[:, :, None, :]; e = rng.integers(0, 4, (N, 8, 15, K)); o = np.argsort(rng.random((N, 8, 15, K)), axis=2)
    v = np.zeros((N, 8, 16, K), np.int64); v[:, :, :15] = b // 15 + (o < b % 15).astype(np.int64) + e - np.roll(e, 1, axis=2); v[:, :, 15] = c
    F = 256 * a + rng.integers(-1, 2, (N, 8, C)); F[..., C - 1] = 256 * a[..., C - 1] + 1
    return v, F
def setup_inputs(rng):
    return pack(records(rng, W), thin(rng, records(rng, K)), names(rng), flows(rng), rng.integers(0, 14001, (N, 8, C)))
def setup_inputs_spread(rng):
    def uneven(k):
        v = np.exp2(2 + 6 * rng.random((N, 8, 1, k))) * rng.random((N, 8, 16, k)); v[:, :, 15] = np.exp2(3 + 5 * rng.random((N, 8, k))) * rng.random((N, 8, k))
        return np.minimum(np.floor(v), 255)
    F = np.minimum(np.floor(np.exp2(16 * rng.random((N, 8, C)))), 61200)
    return pack(uneven(W), uneven(K), names(rng), flows(rng), F)
def setup_inputs_ends(rng):
    mid = 1 + rng.permutation(W - 2); P = np.concatenate([np.array([0, W - 1]), mid[:W // 2 - 2]]); Q = mid[W // 2 - 2:]
    fc = np.zeros(C, bool)
    fc[np.concatenate([np.array([0]), 1 + rng.permutation(C // 2 - 1)])[:C // 4]] = True
    fc[C - 1 - np.concatenate([np.array([0]), 1 + rng.permutation(C // 2 - 1)])[:C // 4]] = True
    fl = np.repeat(fc, 16); L = np.zeros((N, 8, K), np.int64); D = np.zeros((N, 8, W), np.int64)
    for q in range(N):
        for g in range(8):
            D[q, g, P] = rng.permutation(P); D[q, g, Q] = rng.permutation(Q)
            for h in range(2):
                a = np.flatnonzero(fl[h * H:(h + 1) * H]) + h * H; b = np.flatnonzero(~fl[h * H:(h + 1) * H]) + h * H
                p = np.concatenate([P[:2], rng.permutation(P[2:])])[:len(a)]
                L[q, g, a] = p if h == 0 else p[::-1]
                if h == 1:
                    L[q, g, a[-1]] = W - 1; L[q, g, a[-2]] = 0
                L[q, g, b] = rng.permutation(Q)[:len(b)]
    Y = mixed(rng, W); Y[..., P] = 255
    R = np.where(fl[None, None, None, :], 255, mixed(rng, K))
    short = (rng.random((N, 8, C)) < 0.3) & fc[None, None, :]; short[..., 0] = False; short[..., C - 1] = False
    hole = (np.arange(16) == rng.integers(0, 16, (N, 8, C, 1))) & short[..., None]
    R = np.where(hole.reshape(N, 8, 1, K), 0, R)
    near = (rng.random((N, 8, C)) < 0.25) & fc[None, None, :] & ~short; near[..., 0] = False; near[..., C - 1] = False
    R = np.where(lanes(near), 255 - (rng.random((N, 8, 16, K)) < 0.3).astype(np.int64), R)
    F = np.where(fc[None, None, :], np.where(near, 0, 61200), 61200 * rng.integers(0, 2, (N, 8, C)))
    far = int(rng.integers(1, N - 1)); m = rng.integers(1, 17, (8, C)); m[:, 0] = 3; m[:, C - 1] = 16
    live = (np.argsort(rng.random((8, C, 16)), axis=2) < m[..., None]).reshape(8, 1, K)
    z = ((np.arange(16)[None, :, None] == rng.integers(0, 15, (8, 1, K))) & live).astype(np.int64)
    R[far] = np.where(fl[None, None, :], z, R[far]); F[far] = np.where(fc[None, :], 0, 61200)
    return pack(Y, R, L, D, F)
def setup_inputs_corners(rng):
    s = np.arange(W); L = np.zeros((N, 8, K), np.int64); D = np.zeros((N, 8, W), np.int64)
    for q in range(N):
        for g in range(8):
            o = rng.permutation(W); cyc = np.zeros(W, np.int64); cyc[o] = np.roll(o, -1)
            D[q, g] = (s, (s + 1) % W, W - 1 - s, (s - 1) % W, cyc)[(q + g) % 5]
            A, B = ((s[:H], s[W - H:]), (s[0:2 * H:2], s[1:2 * H:2]), (s[W - H:], s[W - H:]), (rng.permutation(W)[:H], rng.permutation(W)[:H]))[(q + 3 * g) % 4]
            L[q, g, :H] = rng.permutation(A); L[q, g, H:] = rng.permutation(B)
    Y = rng.integers(30, 256, (N, 8, 16, W))
    Y[:, :, 15] = np.where(rng.random((N, 8, W)) < 0.7, rng.integers(14, 17, (N, 8, W)), rng.integers(0, 256, (N, 8, W)))
    Y = Y * (rng.random((N, 8, 1, W)) > 0.03125)
    kc = rng.integers(0, 4, (N, 8, C)); m = rng.choice(np.array([0, 1, 2, 15, 16, 16]), (N, 8, C))
    R = np.where(lanes(kc) < 2, steady(rng, 2, 14, 17) * alive(rng, m), records(rng, K))
    F = m * rng.choice(np.array([224, 240]), (N, 8, C)) + rng.integers(0, 2, (N, 8, C))
    F = np.where(kc < 2, F, np.where(kc == 2, rng.integers(0, 14001, (N, 8, C)), 61200 * rng.integers(0, 2, (N, 8, C))))
    return pack(Y, R, L, D, F)
def setup_inputs_crowd(rng):
    o = rng.permutation(W); L = np.zeros((N, 8, K), np.int64)
    for q in range(N):
        for g in range(8):
            L[q, g, :H] = rng.permutation(o[:H]); j = H + rng.integers(0, H)
            if q % 2 == 0:
                L[q, g, H:] = rng.permutation(o[:H])
                if g % 2 == 1: L[q, g, j] = o[rng.integers(H, W)]
            else:
                L[q, g, H:] = rng.permutation(o[H:])[:H]
                if g % 2 == 1: L[q, g, j] = o[rng.integers(0, H)]
    Y = records(rng, W); R = thin(rng, records(rng, K)); F = rng.integers(0, 14001, (N, 8, C))
    high = rng.integers(250, 256, (N, 8, 16, W - H)); high[:, :, 15] = rng.integers(232, 256, (N, 8, W - H)); Y[..., o[H:]] = high
    v, u = strong(rng); R[1::2, :, :, H:] = v[1::2, :, :, H:]; F[1::2, :, C // 2:] = u[1::2, :, C // 2:]
    return pack(Y, R, L, flows(rng), F)
def setup_inputs_calm(rng):
    Y = rng.integers(64, 256, (N, 8, 16, W)); Y[:, :, 15] = rng.integers(60, 256, (N, 8, W))
    m = rng.integers(0, 4, (N, 8, C)); pc = rng.random((N, 8, C)) < 0.25
    R = np.where(lanes(pc), records(rng, K), steady(rng, 4, 60, 256) * alive(rng, m))
    F = np.where(pc, rng.integers(0, 14001, (N, 8, C)), 480 * m + rng.integers(0, 2, (N, 8, C)))
    return pack(Y, R, names(rng), flows(rng), F)
def check_ranges(d):
    bad = []
    for k, lo, hi in (("wl", 0, 255), ("rc", 0, 255), ("nm", 0, W - 1), ("dn", 0, W - 1), ("pl", 0, 61200)):
        v = np.asarray(d[k]).astype(np.float64)
        if not (np.min(v) >= lo and np.max(v) <= hi): bad.append("range of " + k)
        elif np.any(v != np.floor(v)): bad.append("whole numbers of " + k)
    if not bad:
        if np.any(np.sort(d["dn"], axis=-1) != np.arange(W)): bad.append("a row of dn doesn't hold every site once")
        s = np.sort(np.stack([gentries(a) for a in d["nm"]]).reshape(N, 8, 2, H), axis=-1)
        if np.any(s[..., 1:] == s[..., :-1]): bad.append("names of a half in nm repeat")
    return bad
def turn(a, t):
    b = np.roll(a, t, axis=0); h = b.shape[-1] // 2
    b[..., h:] = np.roll(b[..., h:], S * t, axis=1)
    return b
def reference(wl, rc, nm, dn, pl):
    Y = wl.astype(np.float32).astype(np.int32).reshape(N, 8, 16, W); R = rc.astype(np.float32).astype(np.int32).reshape(N, 8, 16, K)
    L = np.stack([gentries(a) for a in nm]).astype(np.int64); D = dn.astype(np.int64); F = np.repeat(pl.astype(np.int64), 16, axis=2)
    E = np.zeros((N, 8, 16, C))
    for t in range(1, T + 1):
        R = turn(R, t); L = turn(L, t); pull = turn(F, t)
        ca = np.zeros((N, 8, W), np.int32); cb = np.zeros((N, 8, W), np.int32)
        np.put_along_axis(ca, L[..., :H], 1, 2); np.put_along_axis(cb, L[..., H:], 1, 2); cnt = ca + cb
        y = np.take_along_axis(Y, L[:, :, None, :], 3)
        b = np.add.reduce(np.minimum(R, y)[:, :, :15], axis=2).astype(np.int64); bond = b > 0
        n = np.repeat(np.add.reduce(bond.reshape(N, 8, C, 16).astype(np.int64), axis=3), 16, axis=2)
        ly = 16 * y[:, :, 15].astype(np.int64); lr = 16 * R[:, :, 15].astype(np.int64); la = np.minimum(ly, lr)
        fail = bond & (n * np.minimum(b, la) < pull); hold = bond & ~fail
        x = np.where(hold[:, :, None, :], EX[np.abs(R - y)], 0.0)
        E = E + turn(np.add.reduce(x.reshape(N, 8, 16, C, 16), axis=4), -t)
        swap = fail & (np.take_along_axis(cnt, L, 2) == 1) & (b > la)
        lig = (swap & (ly <= lr))[:, :, None, :]; rec = (swap & (ly > lr))[:, :, None, :]
        v = np.where(lig, 0, np.where(rec, R, y)); R = np.where(lig, y, np.where(rec, 0, R))
        np.put_along_axis(Y, L[:, :, None, :], v, 3)
        if t < T:
            d = np.take_along_axis(D, L, 2)
            L = np.where(~hold & (np.take_along_axis(cnt, d, 2) == 0), d, L)
        R = turn(R, -t); L = turn(L, -t)
    a = Y.reshape(N, 128, 4, W // 4); r = R.reshape(N, 128, 4, K // 4)
    return {"ye": E.reshape(N, 128, C).astype(np.float32),
            "yw": (a[:, :, 0] - a[:, :, 1] + 2 * a[:, :, 2] - 2 * a[:, :, 3]).astype(np.float32),
            "yr": (r[:, :, 0] - r[:, :, 1] + 2 * r[:, :, 2] - 2 * r[:, :, 3]).astype(np.float32)}

def check_inputs(d):
    bad = list(check_ranges(d))
    if not bad:
        for name, y in reference(**d).items():
            for q in range(N):
                v = np.abs(np.asarray(y[q], np.float64)); s = np.sqrt(np.mean(v * v))
                if v.max() > 10 * s or s < 2.0 ** -3: bad.append('%s of rank %d is uneven or too small' % (name, q))
    return bad

@@ -1,0 +1,519 @@
+from concourse.mybir import AluOpType as ALU
+from concourse.mybir import ActivationFunctionType as AF
+
+W, C, K, H = 4096, 192, 3072, 1536
+HC = C // 2
+STEPS = 3
+SH = 48
+RZ, RD, RC, RB, RBL, RL = 0, 3, 4, 7, 8, 9
+NROLE = 10
+BIG = 131072.0
+GQ, SQ = 2, 3
+ORDER = [
+    57,27,87,28,29,55,33,56,43,35,44,50,30,31,34,45,58,36,46,59,47,52,51,49,48,1,37,42,54,61,81,79,80,53,32,39,68,38,69,60,113,63,4,72,62,65,73,64,41,3,66,114,120,67,-122,123,127,70,75,77,116,40,71,2,147,124,125,126,6,115,94,83,128,133,92,131,5,84,132,117,78,135,157,85,149,76,134,150,130,136,160,158,88,137,138,7,161,151,159,165,152,162,164,82,106,167,108,140,86,111,93,139,141,89,166,107,168,142,163,100,169,143,195,172,154,112,101,145,109,95,171,170,173,121,153,97,144,129,196,155,176,-175,174,74,215,216,239,-182,217,110,183,146,148,90,177,178,102,179,96,103,218,184,119,219,208,180,91,185,197,-222,118,98,186,220,156,181,187,240,223,198,188,189,9,-209,207,-248,249,241,210,211,250,199,221,201,212,213,200,194,253,251,256,14,191,190,247,202,228,193,225,224,252,226,214,227,230,254,13,12,192,-277,278,282,255,10,276,11,229,245,243,260,246,203,262,244,283,284,291,261,259,232,289,264,99,263,268,285,270,279,258,290,266,267,231,293,15,269,288,23,233,204,234,292,295,205,296,294,206,271,257,274,280,297,272,281,298,303,326,299,286,265,327,307,330,300,273,301,331,302,304,275,346,305,105,347,-306,328,314,348,104,-313,308,309,349,329,310,311,339,350,312,315,316,-340,332,351,235,341,317,352,318,242,372,287,353,338,342,17,343,319,-322,370,356,344,-379,380,378,357,21,386,345,381,382,20,323,406,358,320,236,333,383,321,384,385,359,354,19,324,387,375,360,-355,325,18,388,390,22,374,361,362,363,334,407,392,408,414,373,412,413,415,416,391,389,393,396,394,397,377,398,418,399,364,400,376,395,401,402,420,417,409,365,445,447,419,335,366,448,422,421,423,237,446,371,424,410,425,426,427,428,432,451,452,429,449,430,450,238,403,431,433,405,404,411,453,457,458,336,435,-434,466,459,367,-337,467,-368,369,436,460,437,480,461,438,439,-463,440,482,462,-442,481,472,441,483,469,489,484,8,485,468,470,475,-490,465,464,-443,454,471,486,473,491,487,455,476,-444,-496,500,503,26,-502,456,474,477,501,494,-478,16,-493,25,479,507,24,495,508,492,504,488,505,497,506,498,499,509]
+
+bf, f32, i32, u16 = "bfloat16", "float32", "int32", "uint16"
+SCRATCH = {
+    "BW": ("sbuf", [128, W + 3 * K], bf), "OW": ("sbuf", [128, W], bf), "CC": ("sbuf", [128, 3 * K], bf),
+    "RW": ("sbuf", [128, 19 * H], bf), "XG": ("sbuf", [128, K], bf), "XC": ("sbuf", [128, H], bf),
+    "X4": ("sbuf", [128, K], bf), "MM": ("sbuf", [128, 2 * K], bf), "RS": ("sbuf", [128, 2 * K], bf),
+    "STG": ("sbuf", [128, 2 * H], bf), "XE": ("sbuf", [128, 2 * K], f32), "MK": ("sbuf", [128, 2048], bf),
+    "WR": ("sbuf", [128, NROLE * 144], bf), "DF": ("sbuf", [128, 256], f32), "DB": ("sbuf", [128, 896], bf),
+    "SEL": ("sbuf", [128, 256], f32), "BO": ("sbuf", [128, 128], bf), "JD": ("sbuf", [128, 768], bf),
+    "NI": ("sbuf", [128, C], i32), "NL": ("sbuf", [128, C], i32), "LU": ("sbuf", [128, 3 * C], u16),
+    "NP": ("sbuf", [128, 2 * C], u16), "LF": ("sbuf", [128, C], f32), "PU": ("sbuf", [128, C], u16),
+    "DU": ("sbuf", [128, C], u16), "IU": ("sbuf", [128, C], u16), "PFU": ("sbuf", [128, 256], u16),
+    "DI": ("sbuf", [128, 768], i32), "DD": ("sbuf", [128, 512], bf), "PLI": ("sbuf", [128, C], i32),
+    "PLF": ("sbuf", [128, C], f32), "FS": ("sbuf", [128, 3 * C], f32), "FL": ("sbuf", [128, 3 * C], f32),
+    "EI": ("sbuf", [128, 64], i32), "EF": ("sbuf", [128, 64], f32), "SF": ("sbuf", [128, 256], f32),
+    "CJ": ("sbuf", [128, HC], f32), "PF": ("sbuf", [128, 256], f32),
+    "TP": ("sbuf", [128, C], f32), "DDF": ("sbuf", [128, C], f32), "G1": ("sbuf", [128, C], f32),
+    "WW": ("sbuf", [128, C], f32), "FB": ("sbuf", [128, C], f32), "UU": ("sbuf", [128, C], f32),
+    "LE": ("sbuf", [128, C], f32),
+    "GT": ("sbuf", [128, C], bf), "SG": ("sbuf", [128, C], bf), "SW": ("sbuf", [128, C], bf), "AL": ("sbuf", [128, C], bf),
+    "NB": ("sbuf", [128, C], bf), "BD": ("sbuf", [128, C], bf), "NH": ("sbuf", [128, C], bf),
+    "ES": ("sbuf", [128, 3 * C], f32), "EL": ("sbuf", [128, 4 * C], f32),
+    "YS": ("sbuf", [128, 768], f32), "YL": ("sbuf", [128, 768], f32), "YW": ("sbuf", [128, 1024], f32),
+}
+for _b in range(8):
+    SCRATCH["P%d" % _b] = ("psum", [128, 512], f32)
+SEMAPHORES = (["cv", "cs", "ct", "cg", "sent", "outs", "ayr0", "ayr1"] + ["d%d" % _i for _i in range(72)]
+              + ["a%s%d" % (_k, _t) for _k in "nmabcdfe" for _t in range(3)])
+COUNTER = {"v": "cv", "s": "cs", "t": "ct", "g": "cg"}
+PLAN = {}
+
+
+def _clash(a, b):
+    return a[0] == b[0] and a[1] < b[2] and b[1] < a[2] and bool(a[3] & b[3])
+
+
+def _hit(o, p):
+    if not (o["names"] & p["names"]):
+        return False
+    return (any(_clash(a, b) for a in o["w"] for b in p["r"] + p["w"])
+            or any(_clash(a, b) for a in o["r"] for b in p["w"]))
+
+
+def _plan(ops):
+    code = ORDER or list(range(1, len(ops) + 1))
+    order = [abs(x) - 1 for x in code]
+    queue = [op["q"] for op in ops]
+    for x in code:
+        if queue[abs(x) - 1] == "x":
+            queue[abs(x) - 1] = "v" if x < 0 else "s"
+    known = {q: set() for q in "vstgy"}
+    before = {q: set() for q in "vstgy"}
+    seen, waits, need = {}, {}, set()
+    for x, i in enumerate(order):
+        op, q = ops[i], queue[i]
+        if q is None:
+            seen[i] = {i}
+            continue
+        ds = {m for m in range(i) if _hit(ops[m], op)}
+        ds |= {m for m in order[:x] if queue[m] != q and ops[m]["ps"] & op["ps"]}
+        waits[i] = []
+        for m in reversed(order[:x]):
+            if m in ds and m not in known[q] and not (q == "t" and queue[m] == "t"):
+                waits[i].append(m)
+                need.add(m)
+                known[q] |= seen[m]
+        seen[i] = set(known[q]) | {i}
+        if op["kind"] == "c":
+            seen[i] |= before[q]
+            before[q].add(i)
+    return order, queue, waits, need
+
+
+def _emit(g, T, ops):
+    if "plan" not in PLAN:
+        PLAN["plan"] = _plan(ops)
+    order, queue, waits, need = PLAN["plan"]
+    eng = {"v": g.vector, "s": g.scalar, "t": g.tensor, "g": g, "y": g.sync}
+    count = {q: 0 for q in COUNTER}
+    nd, total = 0, {"sent": 0, "outs": 0}
+    for i in order:
+        op, q = ops[i], queue[i]
+        if q is None:
+            continue
+        for m in waits[i]:
+            s, v = ops[m]["tok"]
+            eng[q].wait_ge(T.sem[s], v)
+        if op["kind"] == "c":
+            call = op["fn"](q)
+            if i in need:
+                count[q] += 1
+                call.then_inc(T.sem[COUNTER[q]], 1)
+                op["tok"] = (COUNTER[q], count[q])
+            continue
+        n = 16 if op["kind"] == "d" else op["n"]
+        if i in need:
+            s = "d%d" % nd
+            nd += 1
+            op["tok"] = (s, n)
+        else:
+            s = "outs" if op["kind"] == "d" else "sent"
+            total[s] += n
+        if op["kind"] == "d":
+            op["fn"](q).then_inc(T.sem[s], 16)
+        else:
+            op["fn"](T.sem[s])
+    g.wait_ge(T.sem["sent"], total["sent"])
+    g.sync.wait_ge(T.sem["outs"], total["outs"])
+
+
+def rank_program(g, core, T, topo):
+    rank = T.rank_of(core)
+    if rank is None:
+        return
+    N = len(T.cores)
+    ops = []
+    ALLP = frozenset(range(128))
+
+    def A(name, c0=None, c1=None, step=1, p=None):
+        t = T[name]
+        c0 = 0 if c0 is None else c0
+        c1 = t.shape[1] if c1 is None else c1
+        ps = slice(0, 128) if p is None else slice(*p)
+        cs = slice(c0, c1) if step == 1 else slice(c0, c1, step)
+        return (t[ps, cs], (name, c0, c1, ALLP if p is None else frozenset(range(128)[ps])), len(range(c0, c1, step)))
+
+    def add(q, kind, fn, r, w, **kw):
+        r = [x[1] for x in r if isinstance(x, tuple)]
+        w = [x[1] for x in w]
+        op = {"q": q, "kind": kind, "fn": fn, "r": r, "w": w, "names": frozenset(x[0] for x in r + w),
+              "ps": frozenset(x[0] for x in r + w if SCRATCH[x[0]][0] == "psum")}
+        op.update(kw)
+        ops.append(op)
+
+    def val(x):
+        return x[0] if isinstance(x, tuple) else x
+
+    def ind(win, off):
+        return win[0].indirect(off[0])
+
+    def copy(out, in_):
+        add("v", "c", lambda q: g.vector.tensor_copy(out[0], in_[0]), [in_], [out])
+
+    def tt(out, a, b, op):
+        add("v", "c", lambda q: g.vector.tensor_tensor(out[0], a[0], b[0], op), [a, b], [out])
+
+    def ts(out, a, s1, op0, s2=None, op1=None):
+        if op1 is None:
+            add("v", "c", lambda q: g.vector.tensor_scalar(out[0], a[0], val(s1), None, op0), [a, s1], [out])
+        else:
+            add("v", "c", lambda q: g.vector.tensor_scalar(out[0], a[0], val(s1), val(s2), op0, op1), [a, s1, s2], [out])
+
+    def fill(out, c):
+        add("v", "c", lambda q: g.vector.memset(out[0], c), [], [out])
+
+    def act(out, in_, func, bias=0.0, scale=1.0):
+        add("s", "c", lambda q: g.scalar.activation(out[0], in_[0], func, bias=val(bias), scale=val(scale)),
+            [in_, bias, scale], [out])
+
+    def evac(out, in_):
+        def fn(q):
+            if q == "v":
+                return g.vector.tensor_copy(out[0], in_[0])
+            return g.scalar.activation(out[0], in_[0], AF.Copy)
+        add("x", "c", fn, [in_], [out])
+
+    def gather(out, win, off, mul=None, plus=None, empty=False):
+        def fn(q):
+            if q == "s":
+                if empty:
+                    return g.scalar.activation(out[0], ind(win, off), AF.Relu, bias=1.0, scale=-1.0)
+                if mul is None:
+                    return g.scalar.activation(out[0], ind(win, off), AF.Copy)
+                return g.scalar.activation(out[0], ind(win, off), AF.Identity, bias=plus[0], scale=mul[0])
+            if empty:
+                return g.vector.tensor_scalar(out[0], ind(win, off), 0.0, None, ALU.is_equal)
+            if mul is None:
+                return g.vector.tensor_copy(out[0], ind(win, off))
+            return g.vector.tensor_scalar(out[0], ind(win, off), mul[0], plus[0], ALU.mult, ALU.add)
+        add("x", "c", fn, [win, off, mul, plus], [out])
+
+    def pieces(n):
+        return [(HC * j // n, HC * (j + 1) // n) for j in range(n)]
+
+    def mm(items, first=True, last=True, bank=None):
+        def fn(q):
+            r = None
+            for grp in items:
+                for n, (o, l, x) in enumerate(grp):
+                    r = g.tensor.matmul(o[0], l[0], x[0], first and n == 0, last and n == len(grp) - 1)
+            return r
+        add("t", "c", fn, [y for grp in items for it in grp for y in it[1:]],
+            [bank] if bank else [it[0] for grp in items for it in grp])
+
+    def extract(out, role, name, c0, more=()):
+        mm([[(out, A("WR", role * 144 + 15 - k, role * 144 + 143 - k), A(name, c0 + k, c0 + 16 * out[2], 16))
+             for k in range(16)] + list(more)])
+
+    def iota(out, pattern, base, cm):
+        if SCRATCH[out[1][0]][2] == i32:
+            add("g", "c", lambda q: g.iota(out[0], pattern, base, cm), [], [out])
+        else:
+            add("g", "c", lambda q: g.iota(out[0], pattern, base, cm, allow_small_or_imprecise_dtypes=True), [], [out])
+
+    def sel(buf, pattern, op, fillv, base, cm):
+        add("g", "c", lambda q: g.affine_select(buf[0], buf[0], pattern, op, fillv, base, cm), [buf], [buf])
+
+    def dma(q, out, in_, after=None):
+        eng = g.sync if q == "y" else g.scalar
+        add(q, "d", lambda q: eng.dma_start(val(out), val(in_)), [in_, after], [out] if isinstance(out, tuple) else [])
+
+    def engines(src, dst, small):
+        e = topo.engines(src, dst)
+        return e[::len(e) // 8] if small else e
+
+    def send(hop, out, in_, sem, small):
+        dst = T.cores[(rank + hop) % N]
+        rid, pid, _ = topo.addr(dst)
+        e = engines(core, dst, small)
+        mask = sum(1 << x for x in e)
+        add("g", "r", lambda ls: g.remote_dma(out[0], in_[0], T.sem[sem], ls, pid, rid, mask), [in_], [],
+            n=len(e), sem=sem)
+
+    def arrive(hop, out, sem, small):
+        src = T.cores[(rank - hop) % N]
+        add(None, "a", None, [], [out], tok=(sem, len(engines(src, core, small))))
+
+    def reg(t, h, j):
+        return (3 * (2 * t + h) + j) * H
+
+    def mo(t, h):
+        return (t % 2) * K + h * H
+
+    def half(name, h, base=0):
+        return A(name, base + h * HC, base + (h + 1) * HC)
+
+    def landing(t, h, j):
+        name, o = ("STG", (t - 1) * H) if t and h else ("RW", reg(t, h, 1))
+        return A(name, o + j * H // 2, o + (j + 1) * H // 2)
+
+    def records(t, h, j):
+        o = mo(t, h) + j * H // 2
+        send(1, landing(t, h, j), A("RS", o, o + H // 2), "a%s%d" % ("abcd"[2 * h + j], t), False)
+
+    def wr(r0, n):
+        return A("WR", r0 * 144 + 15, (r0 + n) * 144, 16)
+
+    def db(j):
+        return A("DB", j, j + 128)
+
+    IDB, NEG, WIDE, TWO, NTWO = 0, 128, 256, 384, 640
+    MASKC, BIASC, G16 = 16, 20, 24
+
+    for t in range(STEPS):
+        for h in range(2):
+            arrive(1, half("LU", h, t * C) if t else half("NL", h), "a%s%d" % ("nm"[h], t), True)
+            for j in range(2):
+                arrive(1, landing(t, h, j), "a%s%d" % ("abcd"[2 * h + j], t), False)
+        arrive(t + 1, A("FL", t * C, (t + 1) * C), "af%d" % t, True)
+        arrive(-(t + 1), A("EL", t * C, (t + 1) * C), "ae%d" % t, True)
+    for j in range(2):
+        arrive(-STEPS, A("YL", j * 384, (j + 1) * 384), "ayr%d" % j, False)
+
+    dma("y", A("NI", 0, HC), T.nm[:, 0:HC])
+    dma("s", A("DI", 0, 256), T.dn[:])
+    dma("y", A("NI", HC, C, p=(SH, 128)), T.nm[0:128 - SH, HC:C])
+    dma("s", A("NI", HC, C, p=(0, SH)), T.nm[128 - SH:128, HC:C])
+    dma("y", A("RS", 0, H), T.rc[:, 0:H])
+    dma("y", A("BW", 0, W), T.wl[:])
+    dma("s", A("PLI", p=(0, 8)), T.pl[:])
+    dma("y", A("RS", H, K, p=(SH, 128)), T.rc[0:128 - SH, H:K])
+    dma("y", A("RS", H, K, p=(0, SH)), T.rc[128 - SH:128, H:K])
+    send(1, half("NL", 0), half("NI", 0), "an0", True)
+    send(1, half("NL", 1), half("NI", 1), "am0", True)
+    for j in range(4):
+        records(0, j // 2, j % 2)
+
+    fill(A("RW", 0, H), 0.0)
+    fill(A("OW"), 0.0)
+    ts(A("DI", 256, 512), A("DI", 0, 256), 127, ALU.bitwise_and)
+    ts(A("DI", 512, 768), A("DI", 0, 256), 7, ALU.logical_shift_right)
+    copy(A("DD"), A("DI", 256, 768))
+    dma("s", A("OW", p=(11, 128, 16)), A("DD", 0, 256))
+    dma("y", A("OW", p=(12, 128, 16)), A("DD", 256, 512))
+    iota(A("JD", 0, 384, p=(0, 64)), [[0, 3], [1, 128]], 0, 0)
+    iota(A("JD", 384, 768, p=(0, 64)), [[1, 3], [0, 128]], 0, 3)
+    fill(A("CC", 0, H), 0.0)
+    fill(A("CC", H, K), 0.0)
+    dma("s", A("CC", 0, K, p=(2, 128, 16)), A("JD", 0, 384, p=(0, 64)))
+    dma("y", A("CC", 0, K, p=(3, 128, 16)), A("JD", 384, 768, p=(0, 64)))
+    iota(A("EI", 0, 16), [[-1, 16]], 16, 1)
+    iota(A("EI", 32, 33), [[0, 1]], 0, 1)
+    iota(A("EF", 28, 31), [[24, 3]], 32, 0)
+    ts(A("EI", 16, 32), A("EI", 0, 16), 15, ALU.bitwise_and)
+    ts(A("EI", 33, 34), A("EI", 32, 33), 4, ALU.logical_shift_right)
+    ts(A("EF", 0, 16), A("EI", 16, 32), 0.0, ALU.is_equal)
+    ts(A("EF", 25, 26), A("EI", 33, 34), -24.0, ALU.mult)
+    ts(A("EF", G16, G16 + 1), A("EI", 33, 34), -16.0, ALU.mult)
+    tt(A("EF", 32, 35), A("EF", 2, 11, 3), A("EF", 3, 11, 3), ALU.add)
+    ts(A("EF", 36, 39), A("EF", 28, 31), A("EF", 25, 26), ALU.add)
+    ts(A("EF", MASKC, MASKC + 3), A("EF", 32, 35), -1.0, ALU.mult, 1.0, ALU.add)
+    tt(A("EF", 40, 43), A("EF", 36, 39), A("EF", 3, 11, 3), ALU.mult)
+    tt(A("EF", BIASC, BIASC + 3), A("EF", 40, 43), A("EF", 4, 11, 3), ALU.add)
+    act(A("WR"), A("RW", 0, NROLE * 144), AF.Copy)
+    iota(wr(RZ, 4), [[-381, 4], [-2032, 9]], -253, 127)
+    iota(wr(RC, 5), [[0, 45]], 1, 0)
+    iota(wr(RL, 1), [[0, 9]], 16, 0)
+    sel(wr(RZ, 4), [[-3, 4], [-16, 9]], ALU.is_ge, 0.0, -2, 1)
+    sel(wr(RZ, 4), [[3, 4], [16, 9]], ALU.is_ge, 0.0, 3, -1)
+    sel(wr(RC, 3), [[-3, 3], [-16, 9]], ALU.is_equal, 0.0, -4, 1)
+    sel(wr(RBL, 1), [[-16, 9]], ALU.not_equal, -16.0, -15, 1)
+    sel(wr(RL, 1), [[-16, 9]], ALU.is_equal, 0.0, -15, 1)
+    sel(wr(RB, 2), [[0, 2], [-16, 9]], ALU.is_ge, 0.0, 0, 1)
+    sel(wr(RB, 2), [[1, 2], [16, 9]], ALU.is_ge, 0.0, 14, -1)
+    iota(A("SEL", p=(0, 8)), [[0, 256]], 1, 0)
+    sel(A("SEL", p=(0, 8)), [[0, 2], [-1, 8], [0, 16]], ALU.is_equal, 0.0, 0, 1)
+    iota(A("DF"), [[0, 256]], 1, 0)
+    sel(A("DF"), [[0, 2], [-1, 128]], ALU.is_equal, 0.0, 0, 1)
+    iota(A("BO"), [[0, 128]], 1, 0)
+    sel(A("BO"), [[-16, 8], [0, 16]], ALU.is_ge, 0.0, 0, 1)
+    sel(A("BO"), [[16, 8], [0, 16]], ALU.is_ge, 0.0, 15, -1)
+    iota(A("SF"), [[16, 256]], 0, 1)
+    iota(A("CJ"), [[16, HC]], H, 1)
+    for j in range(4):
+        iota(A("MK", j * 512, (j + 1) * 512), [[0, 512]], 8192, 0)
+        sel(A("MK", j * 512, (j + 1) * 512), [[1, 4], [16, 8], [0, 16]], ALU.is_equal, 0.0, 4 * j, -1)
+    for z in range(1, 7):
+        dma("y", A("RW", 3 * z * H, (3 * z + 1) * H), A("RW", 0, H), A("MK", 0, 8) if z < 3 else A("MK", 1024, 1032))
+    for t in range(1, STEPS):
+        dma("y", A("CC", t * K, (t + 1) * K, p=(3 * t, 128)), A("CC", 0, K, p=(0, 128 - 3 * t)), A("MK", 2040, 2048))
+        dma("y", A("CC", t * K, (t + 1) * K, p=(0, 3 * t)), A("CC", 0, K, p=(4, 4 + 3 * t)), A("MK", 2040, 2048))
+    for j, sc in ((IDB, 1.0), (NTWO, -2.0), (NEG, -1.0), (TWO, 2.0), (WIDE, float(H))):
+        n = 256 if j in (TWO, NTWO) else 128
+        act(A("DB", j, j + n), A("DF", 0, n), AF.Copy, scale=sc)
+    act(A("SF"), A("SF"), AF.Identity, bias=A("EF", G16, G16 + 1))
+    act(A("CJ"), A("CJ"), AF.Identity, bias=A("EF", G16, G16 + 1))
+    copy(A("PLF", p=(0, 8)), A("PLI", p=(0, 8)))
+    grp = []
+    for t in range(STEPS):
+        s = (-SH * (t + 1)) % 128
+        bank, c0 = ("P0", t * C) if t < 2 else ("P1", 0)
+        grp.append([(A(bank, c0, c0 + HC), A("SEL", 0, 128, p=(0, 8)), A("PLF", 0, HC, p=(0, 8)))])
+        grp.append([(A(bank, c0 + HC, c0 + C), A("SEL", s, s + 128, p=(0, 8)), A("PLF", HC, C, p=(0, 8)))])
+    mm(grp)
+    evac(A("FS", 0, 2 * C), A("P0", 0, 2 * C))
+    evac(A("FS", 2 * C, 3 * C), A("P1", 0, C))
+    for t in range(STEPS):
+        send(t + 1, A("FL", t * C, (t + 1) * C), A("FS", t * C, (t + 1) * C), "af%d" % t, True)
+
+    def board(t, h):
+        c = h * HC
+        for a, b in pieces(GQ):
+            gather(A("XG", 16 * (c + a), 16 * (c + b)), A("OW"), A("LU", t * C + c + a, t * C + c + b),
+                   A("EF", MASKC + t, MASKC + t + 1), A("EF", BIASC + t, BIASC + t + 1))
+        for a, b in pieces(SQ):
+            mark(t, c + a, c + b)
+        for z in range(t):
+            extract(half("P3", h, z * C), RZ + z, "XG", h * H)
+            tt(half("TP", h), half("P3", h, z * C), half("TP" if z else "LF", h), ALU.max)
+        if t:
+            copy(half("PU", h), half("TP", h))
+        if t < STEPS - 1:
+            extract(half("P4", h), RD, "XG", h * H)
+            copy(half("DU", h), half("P4", h))
+            tt(half("DDF", h), half("P4", h), half("LF", h), ALU.subtract)
+
+    def mark(t, a, b):
+        out, off = A("OW"), A("LU", t * C + a, t * C + b)
+        x, cc = A("XG", 16 * a, 16 * b), A("CC", t * K + 16 * a, t * K + 16 * b)
+        add("v", "c", lambda q: g.vector.tensor_tensor(ind(out, off), x[0], cc[0], ALU.add), [x, cc, off], [out])
+
+    def least(t, h, a, b):
+        out, win = A("MM", mo(t, h) + 16 * a, mo(t, h) + 16 * b), A("BW", 0, W + t * K)
+        off, r = A("PU" if t else "LU", h * HC + a, h * HC + b), A("RW", reg(t, h, 1) + 16 * a, reg(t, h, 1) + 16 * b)
+        add("v", "c", lambda q: g.vector.tensor_tensor(out[0], ind(win, off), r[0], ALU.min), [win, off, r], [out])
+
+    def links(t, h):
+        for a, b in pieces(GQ):
+            gather(A("RW", reg(t, h, 2) + 16 * a, reg(t, h, 2) + 16 * b), A("BW", 0, W + t * K),
+                   A("PU" if t else "LU", h * HC + a, h * HC + b))
+            least(t, h, a, b)
+        extract(half("P6", h), RB, "MM", mo(t, h))
+        extract(half("P7", h), RBL, "MM", mo(t, h))
+        extract(half("P7", h, C), RL, "RW", reg(t, h, 2))
+
+    def hold(t, h):
+        act(half("BD", h), half("P6", h), AF.Sign)
+        act(half("NB", h), half("P6", h), AF.Relu, bias=BIG, scale=-BIG)
+        act(half("G1", h), half("P7", h), AF.Relu)
+        mm([[(half("P3", h), A("BO"), half("BD", h))],
+            [(half("P3", h, C), A("DF", 0, 128), half("FL", h, t * C)), (half("P3", h, C), db(IDB), half("NB", h))]])
+        tt(half("WW", h), half("P6", h), half("G1", h), ALU.subtract)
+        tt(half("FB", h), half("P3", h), half("WW", h), ALU.mult)
+        tt(half("NH", h), half("P3", h, C), half("FB", h), ALU.is_gt)
+        tt(half("LE", h), half("P7", h, C), half("WW", h), ALU.subtract)
+        act(half("GT", h), half("G1", h), AF.Sign)
+        act(half("SG", h), half("LE", h), AF.Sign, bias=0.5, scale=-1.0)
+
+    def move(t, h):
+        c = h * HC
+        tt(half("UU", h), half("NH", h), half("DDF", h), ALU.mult)
+        for a, b in pieces(GQ):
+            gather(A("X4", 16 * (c + a), 16 * (c + b)), A("OW"), A("DU", c + a, c + b), empty=True)
+        extract(half("P5", h, C), RC + t, "X4", h * H)
+        tt(half("UU", h), half("P5", h, C), half("UU", h), ALU.mult)
+        if h:
+            s, o = 128 - SH, half("P4", 1, C)
+            mm([[(o, A("DF", s, s + 128), half("LF", 1)), (o, A("DF", s, s + 128), half("UU", 1))]])
+        else:
+            o = half("UU", 0)
+            tt(o, o, half("LF", 0), ALU.add)
+        copy(half("NP", h, t * C), o)
+        send(1, half("LU", h, (t + 1) * C), half("NP", h, t * C), "a%s%d" % ("nm"[h], t + 1), True)
+
+    def swap(t, h):
+        if not h:
+            for a, b in pieces(GQ):
+                gather(A("XC", 16 * a, 16 * b), A("OW"), A("LU", t * C + a, t * C + b))
+        o = half("P5", h)
+        extract(o, RC + t, "XG" if h else "XC", h * H, [(o, db(NEG), half("GT", h)), (o, db(NEG), half("NH", h))])
+        act(half("SW", h), o, AF.Relu, scale=-1.0)
+        tt(half("AL", h), half("SW", h), half("SG", h), ALU.mult)
+        o = half("P6", h, C)
+        mm([[(o, A("DF", 0, 128), A("CJ")), (o, db(WIDE), half("AL", h))]])
+        copy(half("IU", h), o)
+        o, u = mo(t + 1, h), W + t * K + h * H
+        for j, (a, b) in enumerate(pieces(2)):
+            gather(A("RS", o + 16 * a, o + 16 * b), A("RW", reg(t, h, 0), reg(t, h, 3)), A("IU", h * HC + a, h * HC + b))
+            if t < STEPS - 1:
+                records(t + 1, h, j)
+        for a, b in pieces(GQ):
+            gather(A("BW", u + 16 * a, u + 16 * b), A("RW", reg(t, h, 1), reg(t, h, 4)), A("IU", h * HC + a, h * HC + b))
+
+    def halve(x, n):
+        out, in_ = A("XE", x, x + n), A("XE", x + n, x + 2 * n)
+        add("g", "d", lambda q: g.dma_start(out[0], in_[0], accum_op=ALU.add), [in_, out], [out])
+
+    def totals(t, h):
+        s, x = (SH * (t + 1) * h) % 128, mo(t, h)
+        tail = t == STEPS - 1 and h
+        for i in range(4):
+            bank, grps = "P%d" % (i % 2), []
+            for kk in range(4):
+                k = 4 * i + kk
+                o = A(bank, kk * HC, (kk + 1) * HC)
+                grps.append([(o, db(IDB), A("RW", reg(t, h, 2) + k, reg(t, h, 3), 16)),
+                             (o, db(IDB), A("RW", reg(t, h, 1) + k, reg(t, h, 2), 16)),
+                             (o, db(NTWO), A("MM", mo(t, h) + k, mo(t, h) + H, 16)),
+                             (o, A("MK", k * 128, (k + 1) * 128), half("NH", h))])
+            mm(grps)
+            act(A("XE", x + i * 2 * C, x + (i + 1) * 2 * C), A(bank, 0, 2 * C), AF.Exp, scale=-1.0 / 64)
+            if tail:
+                mm([[(half("P4", h), A("DF", s, s + 128), half("XE", 0, x + k * HC)) for k in range(4 * i, 4 * i + 4)]],
+                   i == 0, i == 3, A("P4"))
+        if not tail:
+            halve(x, 8 * HC)
+            halve(x, 4 * HC)
+            mm([[(half("P2", h), A("DF", s, s + 128), half("XE", 0, x + k * HC)) for k in range(4)]])
+        evac(half("ES", h, t * C), half("P4" if tail else "P2", h))
+        if h:
+            send(-(t + 1), A("EL", t * C, (t + 1) * C), A("ES", t * C, (t + 1) * C), "ae%d" % t, True)
+
+    for t in range(STEPS):
+        for j in range(2 if t else 0):
+            o, u, n = reg(t, 1, 1) + j * H // 2, (t - 1) * H + j * H // 2, H // 2
+            dma("y", A("RW", o, o + n, p=(SH, 128)), A("STG", u, u + n, p=(0, 128 - SH)))
+            dma("y", A("RW", o, o + n, p=(0, SH)), A("STG", u, u + n, p=(128 - SH, 128)))
+        for h in range(2):
+            if t == 0:
+                copy(half("LU", h), half("NL", h))
+            copy(half("LF", h), half("LU", h, t * C) if t else half("NL", h))
+            board(t, h)
+            links(t, h)
+            hold(t, h)
+        for h in range(2):
+            if t < STEPS - 1:
+                move(t, h)
+            swap(t, h)
+            totals(t, h)
+        for j in range(2):
+            c = j * 128
+            extract(A("P2", 256 + c, 384 + c), RZ + t, "OW", 16 * c)
+            tt(A("PF", c, c + 128), A("P2", 256 + c, 384 + c), A("PF" if t else "SF", c, c + 128), ALU.max)
+
+    copy(A("PFU"), A("PF"))
+    s, b = (SH * STEPS) % 128, mo(STEPS, 0)
+    for j in range(2):
+        o, c = A("P%d" % (6 + j), 0, 384), b + j * 384
+        mm([[(o, db(IDB), A("RS", c, c + 384)), (o, db(NEG), A("RS", c + 768, c + 768 + 384)),
+             (o, db(TWO + s), A("RS", c + H, c + H + 384)), (o, db(NTWO + s), A("RS", c + H + 768, c + H + 768 + 384))]])
+        evac(A("YS", j * 384, (j + 1) * 384), o)
+        send(-STEPS, A("YL", j * 384, (j + 1) * 384), A("YS", j * 384, (j + 1) * 384), "ayr%d" % j, False)
+        dma("y", T.yr[:, j * 384:(j + 1) * 384], A("YL", j * 384, (j + 1) * 384))
+    for j in range(2):
+        for u in range(4):
+            c = u * 1024 + j * 512
+            gather(A("CC", c, c + 512), A("BW"), A("PFU", c // 16, c // 16 + 32))
+        o = A("P%d" % (3 + 2 * j))
+        mm([[(o, db(m), A("CC", u * 1024 + j * 512, u * 1024 + j * 512 + 512))
+             for u, m in enumerate((IDB, NEG, TWO, NTWO))]])
+        evac(A("YW", j * 512, (j + 1) * 512), o)
+        dma("y", T.yw[:, j * 512:(j + 1) * 512], A("YW", j * 512, (j + 1) * 512))
+    tt(A("EL", 3 * C, 4 * C), A("EL", 0, C), A("EL", C, 2 * C), ALU.add)
+    tt(A("EL", 3 * C, 4 * C), A("EL", 3 * C, 4 * C), A("EL", 2 * C, 3 * C), ALU.add)
+    dma("y", T.ye[:], A("EL", 3 * C, 4 * C))
+    _emit(g, T, ops)

@@ -1,3 +1,4 @@
+from concourse.bass import DstId, RemoteDMATransfer
 from concourse.mybir import AluOpType as ALU
 from concourse.mybir import ActivationFunctionType as AF
 
@@ -5,41 +6,48 @@ W, C, K, H = 4096, 192, 3072, 1536
 HC = C // 2
 STEPS = 3
 SH = 48
-RZ, RD, RC, RB, RBL, RL = 0, 3, 4, 7, 8, 9
-NROLE = 10
-BIG = 131072.0
+RZ, RD, RC, RB, RG, MB, MG = 0, 3, 4, 7, 8, 9, 10
+NROLE = 11
+RL = 9
 GQ, SQ = 2, 3
-ORDER = [
-    57,27,87,28,29,55,33,56,43,35,44,50,30,31,34,45,58,36,46,59,47,52,51,49,48,1,37,42,54,61,81,79,80,53,32,39,68,38,69,60,113,63,4,72,62,65,73,64,41,3,66,114,120,67,-122,123,127,70,75,77,116,40,71,2,147,124,125,126,6,115,94,83,128,133,92,131,5,84,132,117,78,135,157,85,149,76,134,150,130,136,160,158,88,137,138,7,161,151,159,165,152,162,164,82,106,167,108,140,86,111,93,139,141,89,166,107,168,142,163,100,169,143,195,172,154,112,101,145,109,95,171,170,173,121,153,97,144,129,196,155,176,-175,174,74,215,216,239,-182,217,110,183,146,148,90,177,178,102,179,96,103,218,184,119,219,208,180,91,185,197,-222,118,98,186,220,156,181,187,240,223,198,188,189,9,-209,207,-248,249,241,210,211,250,199,221,201,212,213,200,194,253,251,256,14,191,190,247,202,228,193,225,224,252,226,214,227,230,254,13,12,192,-277,278,282,255,10,276,11,229,245,243,260,246,203,262,244,283,284,291,261,259,232,289,264,99,263,268,285,270,279,258,290,266,267,231,293,15,269,288,23,233,204,234,292,295,205,296,294,206,271,257,274,280,297,272,281,298,303,326,299,286,265,327,307,330,300,273,301,331,302,304,275,346,305,105,347,-306,328,314,348,104,-313,308,309,349,329,310,311,339,350,312,315,316,-340,332,351,235,341,317,352,318,242,372,287,353,338,342,17,343,319,-322,370,356,344,-379,380,378,357,21,386,345,381,382,20,323,406,358,320,236,333,383,321,384,385,359,354,19,324,387,375,360,-355,325,18,388,390,22,374,361,362,363,334,407,392,408,414,373,412,413,415,416,391,389,393,396,394,397,377,398,418,399,364,400,376,395,401,402,420,417,409,365,445,447,419,335,366,448,422,421,423,237,446,371,424,410,425,426,427,428,432,451,452,429,449,430,450,238,403,431,433,405,404,411,453,457,458,336,435,-434,466,459,367,-337,467,-368,369,436,460,437,480,461,438,439,-463,440,482,462,-442,481,472,441,483,469,489,484,8,485,468,470,475,-490,465,464,-443,454,471,486,473,491,487,455,476,-444,-496,500,503,26,-502,456,474,477,501,494,-478,16,-493,25,479,507,24,495,508,492,504,488,505,497,506,498,499,509]
+EPS = 2.0 ** -13
+US = {"plain": 0.0009, "gather": 0.0012, "scatter": 0.0026, "pe": 0.00046, "v": 0.07, "s": 0.1, "wake": 0.12,
+      "dma": 1.8, "gdma": 0.9, "remote": 0.6, "hop": 1.9, "first": 2.8, "margin": 0.5, "local": 1 / 540e3,
+      "near": 1 / 330e3, "far": 1 / 160e3}
+OPT = {"mode": "yyyyyy", "fold": 0, "via": 2, "halve": 1, "plain": 1, "lean": 0.5, "tries": 45000, "seed": 3, "heat": 1.5,
+       "tail": 1}
+CASES = ({"plain": 1.0, "lag": 1.0, "us": 95}, {"scatter": 1.8, "gather": 1.4, "plain": 1.2, "lag": 1.1, "us": 130},
+         {"scatter": 0.7, "gather": 0.8, "plain": 0.95, "lag": 1.25, "us": 95})
 
 bf, f32, i32, u16 = "bfloat16", "float32", "int32", "uint16"
 SCRATCH = {
-    "BW": ("sbuf", [128, W + 3 * K], bf), "OW": ("sbuf", [128, W], bf), "CC": ("sbuf", [128, 3 * K], bf),
-    "RW": ("sbuf", [128, 19 * H], bf), "XG": ("sbuf", [128, K], bf), "XC": ("sbuf", [128, H], bf),
-    "X4": ("sbuf", [128, K], bf), "MM": ("sbuf", [128, 2 * K], bf), "RS": ("sbuf", [128, 2 * K], bf),
-    "STG": ("sbuf", [128, 2 * H], bf), "XE": ("sbuf", [128, 2 * K], f32), "MK": ("sbuf", [128, 2048], bf),
-    "WR": ("sbuf", [128, NROLE * 144], bf), "DF": ("sbuf", [128, 256], f32), "DB": ("sbuf", [128, 896], bf),
-    "SEL": ("sbuf", [128, 256], f32), "BO": ("sbuf", [128, 128], bf), "JD": ("sbuf", [128, 768], bf),
-    "NI": ("sbuf", [128, C], i32), "NL": ("sbuf", [128, C], i32), "LU": ("sbuf", [128, 3 * C], u16),
-    "NP": ("sbuf", [128, 2 * C], u16), "LF": ("sbuf", [128, C], f32), "PU": ("sbuf", [128, C], u16),
-    "DU": ("sbuf", [128, C], u16), "IU": ("sbuf", [128, C], u16), "PFU": ("sbuf", [128, 256], u16),
-    "DI": ("sbuf", [128, 768], i32), "DD": ("sbuf", [128, 512], bf), "PLI": ("sbuf", [128, C], i32),
-    "PLF": ("sbuf", [128, C], f32), "FS": ("sbuf", [128, 3 * C], f32), "FL": ("sbuf", [128, 3 * C], f32),
-    "EI": ("sbuf", [128, 64], i32), "EF": ("sbuf", [128, 64], f32), "SF": ("sbuf", [128, 256], f32),
-    "CJ": ("sbuf", [128, HC], f32), "PF": ("sbuf", [128, 256], f32),
-    "TP": ("sbuf", [128, C], f32), "DDF": ("sbuf", [128, C], f32), "G1": ("sbuf", [128, C], f32),
-    "WW": ("sbuf", [128, C], f32), "FB": ("sbuf", [128, C], f32), "UU": ("sbuf", [128, C], f32),
-    "LE": ("sbuf", [128, C], f32),
-    "GT": ("sbuf", [128, C], bf), "SG": ("sbuf", [128, C], bf), "SW": ("sbuf", [128, C], bf), "AL": ("sbuf", [128, C], bf),
-    "NB": ("sbuf", [128, C], bf), "BD": ("sbuf", [128, C], bf), "NH": ("sbuf", [128, C], bf),
+    "BW": ("sbuf", [128, W + 3 * K], bf), "OW": ("sbuf", [128, W], bf), "CC": ("sbuf", [128, K], bf),
+    "SW": ("sbuf", [128, 14 * H], bf), "LW": ("sbuf", [128, 10 * H], bf), "XG": ("sbuf", [128, K], bf),
+    "DY": ("sbuf", [128, K], bf), "XC": ("sbuf", [128, H], bf), "X4": ("sbuf", [128, K], bf),
+    "MM": ("sbuf", [128, 2 * K], bf), "RS": ("sbuf", [128, K], bf), "XE": ("sbuf", [128, K], f32),
+    "MK": ("sbuf", [128, 2048], bf), "WR": ("sbuf", [128, NROLE * 144], bf), "DF": ("sbuf", [128, 256], f32),
+    "DB": ("sbuf", [128, 1408], bf), "SEL": ("sbuf", [128, 256], f32), "BO": ("sbuf", [128, 128], bf),
+    "JD": ("sbuf", [128, 768], bf), "NI": ("sbuf", [128, C], i32), "NL": ("sbuf", [128, C], i32),
+    "LU": ("sbuf", [128, 6 * C], u16), "LF": ("sbuf", [128, 6 * C], f32), "MO": ("sbuf", [128, 4 * C], f32),
+    "PU": ("sbuf", [128, C], u16), "DU": ("sbuf", [128, C], u16), "IU": ("sbuf", [128, 3 * C], u16),
+    "PFU": ("sbuf", [128, 256], u16), "DI": ("sbuf", [128, 1536], i32), "DD": ("sbuf", [128, 1024], bf),
+    "PLI": ("sbuf", [128, C], i32), "PLF": ("sbuf", [128, C], f32), "FS": ("sbuf", [128, 3 * C], f32),
+    "FL": ("sbuf", [128, 3 * C], f32), "EI": ("sbuf", [128, 64], i32), "EF": ("sbuf", [128, 80], f32),
+    "EB": ("sbuf", [128, 8], bf), "CJ": ("sbuf", [128, HC], f32), "CB": ("sbuf", [128, HC], bf), "PF": ("sbuf", [128, 512], f32),
+    "DDF": ("sbuf", [128, C], f32), "G1": ("sbuf", [128, C], f32), "WW": ("sbuf", [128, C], f32),
+    "UU": ("sbuf", [128, C], f32), "RI": ("sbuf", [128, C], i32),
+    "GT": ("sbuf", [128, C], bf), "EE": ("sbuf", [128, C], bf), "VV": ("sbuf", [128, C], bf),
+    "BD": ("sbuf", [128, C], bf), "NH": ("sbuf", [128, 2 * C], bf),
     "ES": ("sbuf", [128, 3 * C], f32), "EL": ("sbuf", [128, 4 * C], f32),
     "YS": ("sbuf", [128, 768], f32), "YL": ("sbuf", [128, 768], f32), "YW": ("sbuf", [128, 1024], f32),
 }
 for _b in range(8):
     SCRATCH["P%d" % _b] = ("psum", [128, 512], f32)
-SEMAPHORES = (["cv", "cs", "ct", "cg", "sent", "outs", "ayr0", "ayr1"] + ["d%d" % _i for _i in range(72)]
-              + ["a%s%d" % (_k, _t) for _k in "nmabcdfe" for _t in range(3)])
+SEMAPHORES = (["cv", "cs", "ct", "cg", "sent", "outs", "ayr0", "ayr1"] + ["d%d" % _i for _i in range(90)]
+              + ["a%s%d" % (_k, _t) for _k in "nmiabcdfe" for _t in range(3)]
+              + ["h%d" % _i for _i in range(4)] + ["k%d" % _i for _i in range(4)])
 COUNTER = {"v": "cv", "s": "cs", "t": "ct", "g": "cg"}
+SIZE = {bf: 2, u16: 2, f32: 4, i32: 4}
 PLAN = {}
 
 
@@ -54,13 +62,206 @@ def _hit(o, p):
             or any(_clash(a, b) for a in o["r"] for b in p["w"]))
 
 
+def _order(ops, deps):
+    n = len(ops)
+    sender = {op["sem"]: i for i, op in enumerate(ops) if op["kind"] == "r"}
+    pre = [set(deps[i]) | ({sender[op["sem"]]} if op["kind"] == "a" else set()) for i, op in enumerate(ops)]
+    post = [[] for _ in ops]
+    for i in range(n):
+        if "behind" in ops[i]:
+            pre[i].add(ops[i]["behind"])
+        for m in pre[i]:
+            post[m].append(i)
+    wake = US["wake"]
+
+    hold, lag = [op["hold"] for op in ops], [op["lag"] for op in ops]
+    use, banks = [op.get("use", 0.0) for op in ops], [sorted(op["ps"]) for op in ops]
+    soft = [op.get("behind") for op in ops]
+    pre = [sorted(x) for x in pre]
+
+    def gap(spans, t, d, q=None):
+        lo, hi = 0, len(spans)
+        while lo < hi:
+            mid = (lo + hi) // 2
+            if spans[mid][0] < t - 4.0:
+                lo = mid + 1
+            else:
+                hi = mid
+        for a, b, r in spans[lo:]:
+            if a >= t + d:
+                break
+            if b > t and r != q:
+                t = b
+        return t
+
+    def book(spans, x):
+        spans.append(x)
+        if len(spans) > 1 and spans[-2] > x:
+            spans.sort()
+
+    def sweep(turn, side):
+        busy = {x: [] for x in list("vstgyL") + ["P%d" % b for b in range(8)]}
+        queue, start, done = [None] * n, [0.0] * n, [0.0] * n
+        for i in turn:
+            est = 0.0
+            for m in pre[i]:
+                t = start[m] + hold[m] if soft[i] == m else done[m] + wake
+                if t > est:
+                    est = t
+            q = ops[i]["q"]
+            if q is None:
+                start[i], done[i] = est, est + lag[i]
+                continue
+            pick = None
+            for q in side[i] if q == "x" else q:
+                t, lead = est, hold[i] + lag[i] - use[i] - 1.0
+                while True:
+                    u = gap(busy[q], t, hold[i])
+                    for x in banks[i]:
+                        u = gap(busy[x], u, hold[i], q)
+                    if use[i]:
+                        u = gap(busy["L"], u + lead, use[i]) - lead
+                    if u <= t + 1e-9:
+                        break
+                    t = u
+                if pick is None or t + OPT["lean"] < pick[0]:
+                    pick = (t, q)
+            t, q = pick
+            queue[i], start[i], done[i] = q, t, t + hold[i] + lag[i]
+            book(busy[q], (t, t + hold[i], ""))
+            for x in banks[i]:
+                book(busy[x], (t - wake, t + hold[i] + wake, q))
+            if use[i]:
+                book(busy["L"], (t + lead, t + lead + use[i], ""))
+        return queue, start, done
+
+    def replay(order, queue, k):
+        hold, lag, use = k
+        last, bank, done, end, why = {}, {}, [0.0] * n, [0.0] * n, [None] * n
+        line = (0.0, None)
+        for i in order:
+            q, t = queue[i], 0.0
+            if q in last:
+                why[i] = last[q]
+                t = end[why[i]]
+            for m in hard[i]:
+                if done[m] + wake > t:
+                    t, why[i] = done[m] + wake, m
+            for x in banks[i]:
+                m = bank.get(x)
+                if m is not None and queue[m] != q and end[m] + wake > t:
+                    t, why[i] = end[m] + wake, m
+                bank[x] = i
+            end[i] = t = t + hold[i]
+            if q is not None:
+                last[q] = i
+            done[i] = t = t + lag[i]
+            if use[i]:
+                if line[0] + use[i] + 1.0 > t:
+                    done[i], why[i] = line[0] + use[i] + 1.0, line[1]
+                line = (done[i] - 1.0, i)
+        PLAN["why"] = (why, done, end)
+        i, chain = done.index(max(done)), []
+        while why[i] is not None:
+            if why[i] not in hard[i]:
+                chain.append((i, why[i]))
+            i = why[i]
+        return max(done), chain, end
+
+    hard, above = [[m for m in pre[i] if soft[i] != m] for i in range(n)], [0] * n
+    for i in _topological(pre, post):
+        implied = 0
+        for m in hard[i]:
+            implied |= above[m]
+        for m in hard[i]:
+            above[i] |= above[m] | 1 << m
+        hard[i] = [m for m in hard[i] if not implied >> m & 1]
+    cases = [([hold[i] * k.get(ops[i].get("sort"), k["plain"]) for i in range(n)], [x * k["lag"] for x in lag],
+              [x * k["lag"] for x in use]) for k in CASES]
+
+    def judge(key, side):
+        queue, start, done = sweep(sorted(range(n), key=lambda i: key[i]), side)
+        return weigh(sorted(range(n), key=lambda i: (start[i], done[i])), queue)
+
+    def weigh(order, queue):
+        runs = [replay(order, queue, k) for k in cases]
+        return (sum(r[0] / k["us"] * 100 + sum(r[2]) / n / 30 for r, k in zip(runs, CASES)), [r[0] for r in runs],
+                order, queue, [x for r in runs for x in r[1]], [a - b for a, b in zip(runs[0][2], cases[0][0])])
+
+    way = [0.0] * n
+    for i in reversed(_topological(pre, post)):
+        way[i] = hold[i] + lag[i] + wake + max([0.0] + [way[m] for m in post[i]])
+    side = ["sv"] * n
+    best = now = judge([-x for x in way], side)
+    free = [i for i in range(n) if ops[i]["q"] == "x"]
+    seed = [OPT["seed"]]
+
+    def draw(k):
+        seed[0] = (seed[0] * 1103515245 + 12345) % 2 ** 31
+        return (seed[0] >> 8) % k
+
+    def shift(order, i, to):
+        at = order.index(i)
+        near, part = (pre, order[to:at + 1]) if to < at else (post, order[at:to + 1])
+        on, take, todo = set(part), {i}, [i]
+        for m in todo:
+            for x in near[m]:
+                if x in on and x not in take:
+                    take.add(x)
+                    todo.append(x)
+        a, b = [x for x in part if x in take], [x for x in part if x not in take]
+        return order[:to] + a + b + order[at + 1:] if to < at else order[:at] + b + a + order[to + 1:]
+
+    if "start" in OPT:
+        best = now = weigh([abs(x) - 1 for x in OPT["start"]], [
+            ("v" if -(i + 1) in OPT["start"] else "s") if ops[i]["q"] == "x" else ops[i]["q"] for i in range(n)])
+    for it in range(OPT["tries"]):
+        order, queue = now[2], now[3]
+        i, p = now[4][draw(len(now[4]))]
+        how = draw(10)
+        if how < 3:
+            i = (i, p, free[draw(len(free))])[how]
+            if ops[i]["q"] != "x":
+                continue
+            queue = list(queue)
+            queue[i] = "s" if queue[i] == "v" else "v"
+            if draw(2):
+                order = shift(order, i, max(0, min(n - 1, order.index(i) + draw(41) - 20)))
+        elif how < 6:
+            order = shift(order, i, max(0, order.index(p) - (0, 0, 5, 20)[draw(4)]))
+        elif how < 9:
+            order = shift(order, p, min(n - 1, order.index(i) + (0, 0, 5, 20, 60)[draw(5)]))
+        else:
+            i = draw(n)
+            order = shift(order, i, max(0, min(n - 1, order.index(i) + draw(61) - 30)))
+        new = weigh(order, queue)
+        if new[0] <= now[0] + OPT["heat"] * (1 - it / OPT["tries"]) * draw(100) / 100:
+            if it % 8 == 0:
+                new = min(new, weigh(sorted(order, key=lambda m: new[5][m]), queue), key=lambda r: r[0])
+            now = new
+            if new[0] < best[0]:
+                best = new
+    PLAN["us"] = best[1]
+    PLAN["code"] = [-(i + 1) if best[3][i] == "v" and ops[i]["q"] == "x" else i + 1 for i in best[2]]
+    replay(best[2], best[3], cases[OPT.get("show", 0)])
+    PLAN["ops"] = (ops, best[3], hard)
+    return best[2], best[3]
+
+
+def _topological(pre, post):
+    left = [len(x) for x in pre]
+    turn = [i for i in range(len(pre)) if not left[i]]
+    for i in turn:
+        for m in post[i]:
+            left[m] -= 1
+            if not left[m]:
+                turn.append(m)
+    return turn
+
+
 def _plan(ops):
-    code = ORDER or list(range(1, len(ops) + 1))
-    order = [abs(x) - 1 for x in code]
-    queue = [op["q"] for op in ops]
-    for x in code:
-        if queue[abs(x) - 1] == "x":
-            queue[abs(x) - 1] = "v" if x < 0 else "s"
+    deps = [{m for m in range(i) if _hit(ops[m], op)} for i, op in enumerate(ops)]
+    order, queue = _order(ops, deps)
     known = {q: set() for q in "vstgy"}
     before = {q: set() for q in "vstgy"}
     seen, waits, need = {}, {}, set()
@@ -69,8 +270,7 @@ def _plan(ops):
         if q is None:
             seen[i] = {i}
             continue
-        ds = {m for m in range(i) if _hit(ops[m], op)}
-        ds |= {m for m in order[:x] if queue[m] != q and ops[m]["ps"] & op["ps"]}
+        ds = deps[i] | {m for m in order[:x] if queue[m] != q and ops[m]["ps"] & op["ps"]}
         waits[i] = []
         for m in reversed(order[:x]):
             if m in ds and m not in known[q] and not (q == "t" and queue[m] == "t"):
@@ -121,12 +321,51 @@ def _emit(g, T, ops):
     g.sync.wait_ge(T.sem["outs"], total["outs"])
 
 
+def _carrier(T, topo, rank, h):
+    core, nxt = T.cores[rank], T.cores[(rank + 1) % len(T.cores)]
+    if h == 0 and topo.chip(core) == topo.chip(nxt):
+        return None
+    return [c for c in topo.cores_of(core)
+            if T.rank_of(c) is None and topo.die(c) != topo.die(core) and topo.may_write(c, nxt)][h]
+
+
+def _window(t, h, j):
+    return (5 * (t - 1) + (4 - j if h else j)) * H
+
+
+def _hand_on(g, core, T, topo, rank, h):
+    dst = T.cores[(rank + 1) % len(T.cores)]
+    rid, pid, _ = topo.addr(dst)
+    n = len(topo.engines(T.cores[rank], core))
+    blocks = [b for b in range(4) if h or b % 2 < OPT["via"]]
+    for b in blocks:
+        a, o = b * H, (4 + b) * H
+        if h:
+            for q, to, fro in ((g.sync, slice(SH, 128), slice(0, 128 - SH)), (g.scalar, slice(0, SH), slice(128 - SH, 128))):
+                q.wait_ge(T.sem["h%d" % b], n)
+                q.dma_start(T.LW[to, o:o + H], T.LW[fro, a:a + H]).then_inc(T.sem["k%d" % b], 16)
+            g.wait_ge(T.sem["k%d" % b], 32)
+            a = o
+        else:
+            g.wait_ge(T.sem["h%d" % b], n)
+        t, j = 1 + b // 2, b % 2
+        u = _window(t, h, j)
+        g.remote_dma(T.LW[:, u:u + H], T.LW[:, a:a + H], T.sem["a%s%d" % ("abcd"[2 * h + j], t)], T.sem["sent"],
+                     pid, rid, topo.mask(core, dst))
+    if blocks:
+        g.wait_ge(T.sem["sent"], len(blocks) * len(topo.engines(core, dst)))
+
+
 def rank_program(g, core, T, topo):
     rank = T.rank_of(core)
-    if rank is None:
-        return
     N = len(T.cores)
-    ops = []
+    if rank is None:
+        for r in range(N):
+            for h in range(2):
+                if _carrier(T, topo, r, h) == core:
+                    _hand_on(g, core, T, topo, r, h)
+        return
+    ops, tag = [], [None]
     ALLP = frozenset(range(128))
 
     def A(name, c0=None, c1=None, step=1, p=None):
@@ -137,11 +376,12 @@ def rank_program(g, core, T, topo):
         cs = slice(c0, c1) if step == 1 else slice(c0, c1, step)
         return (t[ps, cs], (name, c0, c1, ALLP if p is None else frozenset(range(128)[ps])), len(range(c0, c1, step)))
 
-    def add(q, kind, fn, r, w, **kw):
+    def add(q, kind, fn, r, w, hold, lag=0.0, **kw):
         r = [x[1] for x in r if isinstance(x, tuple)]
         w = [x[1] for x in w]
         op = {"q": q, "kind": kind, "fn": fn, "r": r, "w": w, "names": frozenset(x[0] for x in r + w),
-              "ps": frozenset(x[0] for x in r + w if SCRATCH[x[0]][0] == "psum")}
+              "ps": frozenset(x[0] for x in r + w if SCRATCH[x[0]][0] == "psum"), "hold": hold, "lag": lag,
+              "tag": tag[0]}
         op.update(kw)
         ops.append(op)
 
@@ -151,31 +391,41 @@ def rank_program(g, core, T, topo):
     def ind(win, off):
         return win[0].indirect(off[0])
 
+    def size(x):
+        return SIZE[SCRATCH[x[1][0]][2]]
+
+    def plain(q, xs, k=1.0):
+        if q == "v" and all(size(x) == 2 for x in xs):
+            k /= 2
+        return US[q] + max(64, xs[0][2] * k) * US["plain"]
+
     def copy(out, in_):
-        add("v", "c", lambda q: g.vector.tensor_copy(out[0], in_[0]), [in_], [out])
+        add("v", "c", lambda q: g.vector.tensor_copy(out[0], in_[0]), [in_], [out], plain("v", [out, in_]))
 
     def tt(out, a, b, op):
-        add("v", "c", lambda q: g.vector.tensor_tensor(out[0], a[0], b[0], op), [a, b], [out])
+        k = 2.0 if all(SCRATCH[x[1][0]][0] == "sbuf" for x in (a, b)) else 1.0
+        add("v", "c", lambda q: g.vector.tensor_tensor(out[0], a[0], b[0], op), [a, b], [out], plain("v", [out, a, b], k))
 
     def ts(out, a, s1, op0, s2=None, op1=None):
-        if op1 is None:
-            add("v", "c", lambda q: g.vector.tensor_scalar(out[0], a[0], val(s1), None, op0), [a, s1], [out])
-        else:
-            add("v", "c", lambda q: g.vector.tensor_scalar(out[0], a[0], val(s1), val(s2), op0, op1), [a, s1, s2], [out])
+        more = () if op1 is None else (op1,)
+        add("v", "c", lambda q: g.vector.tensor_scalar(out[0], a[0], val(s1), val(s2), op0, *more), [a, s1, s2], [out],
+            plain("v", [out, a]))
 
     def fill(out, c):
-        add("v", "c", lambda q: g.vector.memset(out[0], c), [], [out])
+        add("v", "c", lambda q: g.vector.memset(out[0], c), [], [out], plain("v", [out]))
 
     def act(out, in_, func, bias=0.0, scale=1.0):
         add("s", "c", lambda q: g.scalar.activation(out[0], in_[0], func, bias=val(bias), scale=val(scale)),
-            [in_, bias, scale], [out])
+            [in_, bias, scale], [out], plain("s", [out]))
 
-    def evac(out, in_):
+    def evac(out, in_, mul=None):
         def fn(q):
-            if q == "v":
+            if q == "s":
+                return g.scalar.activation(out[0], in_[0], AF.Copy, scale=1.0 if mul is None else mul[0])
+            if mul is None:
                 return g.vector.tensor_copy(out[0], in_[0])
-            return g.scalar.activation(out[0], in_[0], AF.Copy)
-        add("x", "c", fn, [in_], [out])
+            return g.vector.tensor_scalar(out[0], in_[0], mul[0], None, ALU.mult)
+        add("x", "c", fn, [in_, mul], [out], plain("s", [out]))
 
     def gather(out, win, off, mul=None, plus=None, empty=False):
         def fn(q):
@@ -190,7 +440,7 @@ def rank_program(g, core, T, topo):
             if mul is None:
                 return g.vector.tensor_copy(out[0], ind(win, off))
             return g.vector.tensor_scalar(out[0], ind(win, off), mul[0], plus[0], ALU.mult, ALU.add)
-        add("x", "c", fn, [win, off, mul, plus], [out])
+        add("x", "c", fn, [win, off, mul, plus], [out], US["v"] + out[2] * US["gather"], sort="gather")
 
     def pieces(n):
         return [(HC * j // n, HC * (j + 1) // n) for j in range(n)]
@@ -203,43 +453,74 @@ def rank_program(g, core, T, topo):
                     r = g.tensor.matmul(o[0], l[0], x[0], first and n == 0, last and n == len(grp) - 1)
             return r
         add("t", "c", fn, [y for grp in items for it in grp for y in it[1:]],
-            [bank] if bank else [it[0] for grp in items for it in grp])
+            [bank] if bank else [it[0] for grp in items for it in grp],
+            sum(max(64, x[2]) * (4 if size(x) == 4 else 1) * US["pe"] for grp in items for _, _, x in grp), sort="pe")
 
-    def extract(out, role, name, c0, more=()):
+    def extract(out, role, name, c0, more=(), **kw):
         mm([[(out, A("WR", role * 144 + 15 - k, role * 144 + 143 - k), A(name, c0 + k, c0 + 16 * out[2], 16))
-             for k in range(16)] + list(more)])
+             for k in range(16)] + list(more)], **kw)
 
     def iota(out, pattern, base, cm):
-        if SCRATCH[out[1][0]][2] == i32:
-            add("g", "c", lambda q: g.iota(out[0], pattern, base, cm), [], [out])
-        else:
-            add("g", "c", lambda q: g.iota(out[0], pattern, base, cm, allow_small_or_imprecise_dtypes=True), [], [out])
+        kw = {} if SCRATCH[out[1][0]][2] == i32 else {"allow_small_or_imprecise_dtypes": True}
+        add("g", "c", lambda q: g.iota(out[0], pattern, base, cm, **kw), [], [out], 0.13 + 2 * out[2] * US["plain"])
 
     def sel(buf, pattern, op, fillv, base, cm):
-        add("g", "c", lambda q: g.affine_select(buf[0], buf[0], pattern, op, fillv, base, cm), [buf], [buf])
+        add("g", "c", lambda q: g.affine_select(buf[0], buf[0], pattern, op, fillv, base, cm), [buf], [buf],
+            0.17 + 2 * buf[2] * US["plain"])
+
+    def span(x):
+        return max(64, len(x[1][3])) * x[2] * size(x)
 
     def dma(q, out, in_, after=None):
         eng = g.sync if q == "y" else g.scalar
-        add(q, "d", lambda q: eng.dma_start(val(out), val(in_)), [in_, after], [out] if isinstance(out, tuple) else [])
+        sides = [x for x in (out, in_) if isinstance(x, tuple)]
+        if min(len(x[1][3]) for x in sides) <= 8:
+            kw = {"lag": US["dma"] + 0.6}
+        else:
+            use = 0.3 + span(sides[0]) * US["local"]
+            kw = {"lag": US["dma"] + use, "on": "L", "use": use}
+        add(q, "d", lambda q: eng.dma_start(val(out), val(in_)), [in_, after], [out] if isinstance(out, tuple) else [],
+            0.06, **kw)
+
+    def accumulate(out, in_):
+        use = 0.3 + 2 * span(out) * US["local"]
+        add("g", "d", lambda q: g.dma_start(out[0], in_[0], accum_op=ALU.add), [in_, out], [out], US["gdma"],
+            US["dma"] + use + US["margin"], on="L", use=use)
 
     def engines(src, dst, small):
         e = topo.engines(src, dst)
         return e[::len(e) // 8] if small else e
 
-    def send(hop, out, in_, sem, small):
-        dst = T.cores[(rank + hop) % N]
+    def write(dst, out, in_, sem, small, landing, on, plus=None):
         rid, pid, _ = topo.addr(dst)
         e = engines(core, dst, small)
         mask = sum(1 << x for x in e)
-        add("g", "r", lambda ls: g.remote_dma(out[0], in_[0], T.sem[sem], ls, pid, rid, mask), [in_], [],
-            n=len(e), sem=sem)
+        use = (0.7 if on == "R" else 0.4) + span(in_) * (US["far" if on == "R" else "near"] + (US["local"] if plus else 0.0))
 
-    def arrive(hop, out, sem, small):
-        src = T.cores[(rank - hop) % N]
-        add(None, "a", None, [], [out], tok=(sem, len(engines(src, core, small))))
+        def fn(ls):
+            if plus is None:
+                return g.remote_dma(out[0], in_[0], T.sem[sem], ls, pid, rid, mask)
+            return g.remote_dma_fused([RemoteDMATransfer(
+                dst_ids=[DstId(rid=rid, pnc=pid)], dma_engine_mask=mask, remote_sem=T.sem[sem],
+                srcs=[in_[0], plus[0]], dsts=[out[0]], alu_op=1)], local_sem=ls)
+        add("g", "r", fn, [in_, plus], [],
+            US["remote"] + (US["first"] if landing == "an0" else 0.0), US["hop"] + use,
+            n=len(e), sem=landing, on="L", use=use)
 
-    def reg(t, h, j):
-        return (3 * (2 * t + h) + j) * H
+    def send(hop, out, in_, sem, small):
+        write(T.cores[(rank + hop) % N], out, in_, sem, small, sem, "R")
+
+    def arrive(src, out, sem, small, lag=0.0):
+        add(None, "a", None, [], [out], 0.0, lag, sem=sem, tok=(sem, len(engines(src, core, small))))
+
+    def behind(hop):
+        return T.cores[(rank - hop) % N]
+
+    def site(t, h, j):
+        return (8 + 3 * h + j if t % 2 else 1 + 4 * h + j) * H
+
+    def block(name, o):
+        return A(name, o, o + H)
 
     def mo(t, h):
         return (t % 2) * K + h * H
@@ -247,13 +528,22 @@ def rank_program(g, core, T, topo):
     def half(name, h, base=0):
         return A(name, base + h * HC, base + (h + 1) * HC)
 
-    def landing(t, h, j):
-        name, o = ("STG", (t - 1) * H) if t and h else ("RW", reg(t, h, 1))
-        return A(name, o + j * H // 2, o + (j + 1) * H // 2)
+    def lists(name, t, h, j=0, a=0, b=HC):
+        o = (2 * t + h) * C + j * HC
+        return A(name, o + a, o + b)
 
     def records(t, h, j):
-        o = mo(t, h) + j * H // 2
-        send(1, landing(t, h, j), A("RS", o, o + H // 2), "a%s%d" % ("abcd"[2 * h + j], t), False)
+        tag[0] = ("pass" if j else "carry", t, h)
+        via, sem = _carrier(T, topo, rank, h), "a%s%d" % ("abcd"[2 * h + j], t + 1)
+        if j and OPT["fold"]:
+            src, plus = block("SW", site(t, h, 2)), block(*dy(t, h))
+        else:
+            src, plus = block("SW", site(t, h, 2 - 2 * j)), None
+        on = "L" if h or j < OPT["via"] else "R"
+        if via is None or on == "R":
+            write(behind(-1), block("LW", _window(t + 1, h, j)), src, sem, False, sem, on, plus)
+        else:
+            write(via, block("LW", (2 * t + j) * H), src, "h%d" % (2 * t + j), False, sem, on, plus)
 
     def wr(r0, n):
         return A("WR", r0 * 144 + 15, (r0 + n) * 144, 16)
@@ -261,70 +551,102 @@ def rank_program(g, core, T, topo):
     def db(j):
         return A("DB", j, j + 128)
 
-    IDB, NEG, WIDE, TWO, NTWO = 0, 128, 256, 384, 640
-    MASKC, BIASC, G16 = 16, 20, 24
+    def col(j, n=1):
+        return A("EF", j, j + n)
+
+    IDB, NEG, BACK, TWO, NTWO, FLAG, HIGH, WIDE = 0, 128, 256, 512, 768, 1024, 1152, 1280
+    MASKC, BIASC, G16, KCOL, LANE = 16, 20, 24, 26, 48
 
     for t in range(STEPS):
         for h in range(2):
-            arrive(1, half("LU", h, t * C) if t else half("NL", h), "a%s%d" % ("nm"[h], t), True)
+            if t == 0:
+                arrive(behind(1), half("NL", h), "a%s0" % "nm"[h], True)
+                arrive(behind(1), block("SW", site(0, h, 2)), "a%s0" % "ac"[h], False)
+                continue
+            arrive(behind(1), lists("LF", t, h, 0, 0, (h + 1) * HC), "a%s%d" % ("nm"[h], t), True)
+            via = _carrier(T, topo, (rank - 1) % N, h)
             for j in range(2):
-                arrive(1, landing(t, h, j), "a%s%d" % ("abcd"[2 * h + j], t), False)
-        arrive(t + 1, A("FL", t * C, (t + 1) * C), "af%d" % t, True)
-        arrive(-(t + 1), A("EL", t * C, (t + 1) * C), "ae%d" % t, True)
+                handed = h or j < OPT["via"]
+                arrive(via if handed and via is not None else behind(1), block("LW", _window(t, h, j)),
+                       "a%s%d" % ("abcd"[2 * h + j], t), False, (5.5 + 2.5 * h) * handed)
+        if t:
+            arrive(behind(1), lists("LU", t, 0, 1), "ai%d" % t, True)
+        arrive(behind(t + 1), A("FL", t * C, (t + 1) * C), "af%d" % t, True)
+        arrive(behind(-(t + 1)), A("EL", t * C, (t + 1) * C), "ae%d" % t, True)
     for j in range(2):
-        arrive(-STEPS, A("YL", j * 384, (j + 1) * 384), "ayr%d" % j, False)
+        arrive(behind(-STEPS), A("YL", j * 384, (j + 1) * 384), "ayr%d" % j, False)
 
+    def in_turn(first):
+        for i in range(first + 1, len(ops)):
+            ops[i]["behind"] = i - 1
+
+    first = len(ops)
     dma("y", A("NI", 0, HC), T.nm[:, 0:HC])
     dma("s", A("DI", 0, 256), T.dn[:])
     dma("y", A("NI", HC, C, p=(SH, 128)), T.nm[0:128 - SH, HC:C])
     dma("s", A("NI", HC, C, p=(0, SH)), T.nm[128 - SH:128, HC:C])
     dma("y", A("RS", 0, H), T.rc[:, 0:H])
-    dma("y", A("BW", 0, W), T.wl[:])
     dma("s", A("PLI", p=(0, 8)), T.pl[:])
     dma("y", A("RS", H, K, p=(SH, 128)), T.rc[0:128 - SH, H:K])
     dma("y", A("RS", H, K, p=(0, SH)), T.rc[128 - SH:128, H:K])
+    dma("y", A("BW", 0, W), T.wl[:])
     send(1, half("NL", 0), half("NI", 0), "an0", True)
+    send(1, block("SW", site(0, 0, 2)), block("RS", 0), "aa0", False)
     send(1, half("NL", 1), half("NI", 1), "am0", True)
-    for j in range(4):
-        records(0, j // 2, j % 2)
+    send(1, block("SW", site(0, 1, 2)), block("RS", H), "ac0", False)
+    in_turn(first)
 
-    fill(A("RW", 0, H), 0.0)
+    zero = block("SW", site(0, 0, 1))
+    fill(zero, 0.0)
     fill(A("OW"), 0.0)
-    ts(A("DI", 256, 512), A("DI", 0, 256), 127, ALU.bitwise_and)
-    ts(A("DI", 512, 768), A("DI", 0, 256), 7, ALU.logical_shift_right)
-    copy(A("DD"), A("DI", 256, 768))
-    dma("s", A("OW", p=(11, 128, 16)), A("DD", 0, 256))
-    dma("y", A("OW", p=(12, 128, 16)), A("DD", 256, 512))
+    iota(A("DI", 256, 512), [[1, 256]], 0, 256)
+    ts(A("DI", 512, 1024), A("DI", 0, 512), 127, ALU.bitwise_and)
+    ts(A("DI", 1024, 1536), A("DI", 0, 512), 7, ALU.logical_shift_right, 31, ALU.bitwise_and)
+    copy(A("DD", 0, 512), A("DI", 512, 1024))
+    copy(A("DD", 512, 1024), A("DI", 1024, 1536))
+    for n, (row, j) in enumerate(((11, 0), (2, 1), (5, 1), (12, 2), (3, 3), (6, 3))):
+        dma("sy"[n % 2], A("OW", p=(row, 128, 16)), A("DD", j * 256, (j + 1) * 256))
     iota(A("JD", 0, 384, p=(0, 64)), [[0, 3], [1, 128]], 0, 0)
     iota(A("JD", 384, 768, p=(0, 64)), [[1, 3], [0, 128]], 0, 3)
     fill(A("CC", 0, H), 0.0)
     fill(A("CC", H, K), 0.0)
-    dma("s", A("CC", 0, K, p=(2, 128, 16)), A("JD", 0, 384, p=(0, 64)))
-    dma("y", A("CC", 0, K, p=(3, 128, 16)), A("JD", 384, 768, p=(0, 64)))
+    for n, row in enumerate((2, 3, 5, 6)):
+        j = 384 * (n % 2)
+        dma("sy"[n % 2], A("CC", 0, K, p=(row, 128, 16)), A("JD", j, j + 384, p=(0, 64)))
     iota(A("EI", 0, 16), [[-1, 16]], 16, 1)
     iota(A("EI", 32, 33), [[0, 1]], 0, 1)
-    iota(A("EF", 28, 31), [[24, 3]], 32, 0)
+    iota(col(28, 3), [[24, 3]], 32, 0)
     ts(A("EI", 16, 32), A("EI", 0, 16), 15, ALU.bitwise_and)
     ts(A("EI", 33, 34), A("EI", 32, 33), 4, ALU.logical_shift_right)
-    ts(A("EF", 0, 16), A("EI", 16, 32), 0.0, ALU.is_equal)
-    ts(A("EF", 25, 26), A("EI", 33, 34), -24.0, ALU.mult)
-    ts(A("EF", G16, G16 + 1), A("EI", 33, 34), -16.0, ALU.mult)
-    tt(A("EF", 32, 35), A("EF", 2, 11, 3), A("EF", 3, 11, 3), ALU.add)
-    ts(A("EF", 36, 39), A("EF", 28, 31), A("EF", 25, 26), ALU.add)
-    ts(A("EF", MASKC, MASKC + 3), A("EF", 32, 35), -1.0, ALU.mult, 1.0, ALU.add)
-    tt(A("EF", 40, 43), A("EF", 36, 39), A("EF", 3, 11, 3), ALU.mult)
-    tt(A("EF", BIASC, BIASC + 3), A("EF", 40, 43), A("EF", 4, 11, 3), ALU.add)
-    act(A("WR"), A("RW", 0, NROLE * 144), AF.Copy)
+    ts(col(0, 16), A("EI", 16, 32), 0.0, ALU.is_equal)
+    ts(col(25), A("EI", 33, 34), -24.0, ALU.mult)
+    ts(col(G16), A("EI", 33, 34), -16.0, ALU.mult)
+    tt(col(32, 3), A("EF", 2, 11, 3), A("EF", 3, 11, 3), ALU.add)
+    ts(col(36, 3), col(28, 3), col(25), ALU.add)
+    ts(col(MASKC, 3), col(32, 3), -1.0, ALU.mult, 1.0, ALU.add)
+    tt(col(MASKC), col(MASKC), col(33), ALU.subtract)
+    tt(col(40, 3), col(36, 3), A("EF", 3, 11, 3), ALU.mult)
+    tt(col(BIASC, 3), col(40, 3), A("EF", 4, 11, 3), ALU.add)
+    ts(col(BIASC), col(6), col(36), ALU.mult, col(BIASC), ALU.add)
+    if "y" not in OPT["mode"]:
+        ts(A("EB", 0, 1), col(15), EPS, ALU.mult)
+    ts(col(LANE, 16), col(0, 16), 8192.0, ALU.mult)
+    copy(col(KCOL), A("EI", 16, 17))
+    act(A("WR", 0, MB * 144), A("SW", site(0, 0, 1), site(0, 0, 1) + MB * 144), AF.Copy)
     iota(wr(RZ, 4), [[-381, 4], [-2032, 9]], -253, 127)
     iota(wr(RC, 5), [[0, 45]], 1, 0)
-    iota(wr(RL, 1), [[0, 9]], 16, 0)
     sel(wr(RZ, 4), [[-3, 4], [-16, 9]], ALU.is_ge, 0.0, -2, 1)
     sel(wr(RZ, 4), [[3, 4], [16, 9]], ALU.is_ge, 0.0, 3, -1)
     sel(wr(RC, 3), [[-3, 3], [-16, 9]], ALU.is_equal, 0.0, -4, 1)
-    sel(wr(RBL, 1), [[-16, 9]], ALU.not_equal, -16.0, -15, 1)
-    sel(wr(RL, 1), [[-16, 9]], ALU.is_equal, 0.0, -15, 1)
+    sel(wr(RG, 1), [[-16, 9]], ALU.not_equal, -16.0, -15, 1)
     sel(wr(RB, 2), [[0, 2], [-16, 9]], ALU.is_ge, 0.0, 0, 1)
     sel(wr(RB, 2), [[1, 2], [16, 9]], ALU.is_ge, 0.0, 14, -1)
+    if "y" in OPT["mode"]:
+        act(A("WR", MB * 144, MG * 144), A("SW", site(0, 0, 1), site(0, 0, 1) + 144), AF.Copy)
+        iota(wr(RL, 1), [[0, 9]], 16, 0)
+        sel(wr(RL, 1), [[-16, 9]], ALU.is_equal, 0.0, -15, 1)
+    else:
+        act(A("WR", MB * 144, NROLE * 144), A("WR", RB * 144, MB * 144), AF.Copy, scale=-0.5)
     iota(A("SEL", p=(0, 8)), [[0, 256]], 1, 0)
     sel(A("SEL", p=(0, 8)), [[0, 2], [-1, 8], [0, 16]], ALU.is_equal, 0.0, 0, 1)
     iota(A("DF"), [[0, 256]], 1, 0)
@@ -332,22 +654,22 @@ def rank_program(g, core, T, topo):
     iota(A("BO"), [[0, 128]], 1, 0)
     sel(A("BO"), [[-16, 8], [0, 16]], ALU.is_ge, 0.0, 0, 1)
     sel(A("BO"), [[16, 8], [0, 16]], ALU.is_ge, 0.0, 15, -1)
-    iota(A("SF"), [[16, 256]], 0, 1)
-    iota(A("CJ"), [[16, HC]], H, 1)
-    for j in range(4):
-        iota(A("MK", j * 512, (j + 1) * 512), [[0, 512]], 8192, 0)
-        sel(A("MK", j * 512, (j + 1) * 512), [[1, 4], [16, 8], [0, 16]], ALU.is_equal, 0.0, 4 * j, -1)
-    for z in range(1, 7):
-        dma("y", A("RW", 3 * z * H, (3 * z + 1) * H), A("RW", 0, H), A("MK", 0, 8) if z < 3 else A("MK", 1024, 1032))
-    for t in range(1, STEPS):
-        dma("y", A("CC", t * K, (t + 1) * K, p=(3 * t, 128)), A("CC", 0, K, p=(0, 128 - 3 * t)), A("MK", 2040, 2048))
-        dma("y", A("CC", t * K, (t + 1) * K, p=(0, 3 * t)), A("CC", 0, K, p=(4, 4 + 3 * t)), A("MK", 2040, 2048))
-    for j, sc in ((IDB, 1.0), (NTWO, -2.0), (NEG, -1.0), (TWO, 2.0), (WIDE, float(H))):
-        n = 256 if j in (TWO, NTWO) else 128
+    iota(A("CJ"), [[16, HC]], 2 * H, 1)
+    iota(A("CB"), [[16, HC]], 0, 0)
+    for k in range(16):
+        evac(A("MK", k * 128, (k + 1) * 128), A("BO"), col(LANE + k))
+    late = block("SW", site(0, 1, 2))
+    act(block("SW", site(0, 1, 1)), zero, AF.Copy)
+    act(block("LW", _window(1, 0, 2)), zero, AF.Copy)
+    for h in range(2):
+        dma("y", block("SW", site(1, h, 1)), zero, late)
+    dma("y", block("LW", _window(2, 0, 2)), zero, late)
+    for j, sc in ((IDB, 1.0), (NEG, -1.0), (FLAG, -0.5 if "y" in OPT["mode"] else -256.0), (WIDE, float(H)), (BACK, -float(H)), (HIGH, 128.0),
+                  (NTWO, -2.0), (TWO, 2.0)):
+        n = 256 if j in (BACK, TWO, NTWO) else 128
         act(A("DB", j, j + n), A("DF", 0, n), AF.Copy, scale=sc)
-    act(A("SF"), A("SF"), AF.Identity, bias=A("EF", G16, G16 + 1))
-    act(A("CJ"), A("CJ"), AF.Identity, bias=A("EF", G16, G16 + 1))
-    copy(A("PLF", p=(0, 8)), A("PLI", p=(0, 8)))
+    act(A("CJ"), A("CJ"), AF.Identity, bias=col(G16))
+    ts(A("PLF", p=(0, 8)), A("PLI", p=(0, 8)), 2.0 ** -20, ALU.max)
     grp = []
     for t in range(STEPS):
         s = (-SH * (t + 1)) % 128
@@ -360,160 +682,245 @@ def rank_program(g, core, T, topo):
     for t in range(STEPS):
         send(t + 1, A("FL", t * C, (t + 1) * C), A("FS", t * C, (t + 1) * C), "af%d" % t, True)
 
+    def pb(h, j):
+        return A("P%d" % (2 + 2 * h), j * HC, (j + 1) * HC)
+
+    def pg(h, j):
+        return A("P%d" % (3 + 2 * h), j * HC, (j + 1) * HC)
+
+    def nh(t, h):
+        return half("NH", h, (t % 2) * C)
+
+    def names(t, h):
+        return lists("LF", t, h) if t else half("NL", h)
+
+    def aside(t, h):
+        return OPT["mode"][2 * t + h] not in "gy"
+
+    def dy(t, h):
+        return ("DY", h * H) if aside(t, h) else ("SW", site(t, h, 0))
+
+    def receptors(t, h):
+        tag[0] = ("take", t, h)
+        if t == 0:
+            copy(lists("LU", 0, h), half("NL", h))
+            if h:
+                copy(lists("LF", 0, h), half("NL", h))
+        else:
+            copy(lists("LU", t, h, 0, 0, (h + 1) * HC), lists("LF", t, h, 0, 0, (h + 1) * HC))
+            o, u = site(t, h, 2), _window(t, h, 2 * h)
+            tag[0] = ("cells", t, h)
+            for a, b in pieces(GQ):
+                gather(A("SW", o + 16 * a, o + 16 * b), A("LW", u, u + 3 * H), lists("LU", t, h, 1, a, b))
+        for j in (0,) * aside(t, h) + (-1,) * (t == STEPS - 1):
+            dma("y", block("SW", site(t, h, j)), block("SW", site(t, h, 2)))
+        if t < STEPS - 1:
+            records(t, h, 0)
+
     def board(t, h):
         c = h * HC
+        tag[0] = ("read", t, h)
         for a, b in pieces(GQ):
-            gather(A("XG", 16 * (c + a), 16 * (c + b)), A("OW"), A("LU", t * C + c + a, t * C + c + b),
-                   A("EF", MASKC + t, MASKC + t + 1), A("EF", BIASC + t, BIASC + t + 1))
+            gather(A("XG", 16 * (c + a), 16 * (c + b)), A("OW"), lists("LU", t, h, 0, a, b), col(MASKC + t), col(BIASC + t))
+        tag[0] = ("mark", t, h)
         for a, b in pieces(SQ):
-            mark(t, c + a, c + b)
-        for z in range(t):
-            extract(half("P3", h, z * C), RZ + z, "XG", h * H)
-            tt(half("TP", h), half("P3", h, z * C), half("TP" if z else "LF", h), ALU.max)
+            mark(t, h, a, b)
+        tag[0] = ("point", t, h)
         if t:
-            copy(half("PU", h), half("TP", h))
+            extract(half("P6", h), RZ + t - 1, "XG", h * H)
+            copy(half("PU", h), half("P6", h))
         if t < STEPS - 1:
-            extract(half("P4", h), RD, "XG", h * H)
-            copy(half("DU", h), half("P4", h))
-            tt(half("DDF", h), half("P4", h), half("LF", h), ALU.subtract)
+            tag[0] = ("down", t, h)
+            extract(half("P6", h, C), RD, "XG", h * H)
+            copy(half("DU", h), half("P6", h, C))
+            tt(half("DDF", h), half("P6", h, C), names(t, h), ALU.subtract)
 
-    def mark(t, a, b):
-        out, off = A("OW"), A("LU", t * C + a, t * C + b)
-        x, cc = A("XG", 16 * a, 16 * b), A("CC", t * K + 16 * a, t * K + 16 * b)
-        add("v", "c", lambda q: g.vector.tensor_tensor(ind(out, off), x[0], cc[0], ALU.add), [x, cc, off], [out])
+    def mark(t, h, a, b):
+        out, off, o = A("OW"), lists("LU", t, h, 0, a, b), h * H
+        x, cc = A("XG", o + 16 * a, o + 16 * b), A("CC", o + 16 * a, o + 16 * b)
+        add("v", "c", lambda q: g.vector.tensor_tensor(ind(out, off), x[0], cc[0], ALU.add), [x, cc, off], [out],
+            US["v"] + x[2] * US["scatter"], sort="scatter")
 
-    def least(t, h, a, b):
-        out, win = A("MM", mo(t, h) + 16 * a, mo(t, h) + 16 * b), A("BW", 0, W + t * K)
-        off, r = A("PU" if t else "LU", h * HC + a, h * HC + b), A("RW", reg(t, h, 1) + 16 * a, reg(t, h, 1) + 16 * b)
-        add("v", "c", lambda q: g.vector.tensor_tensor(out[0], ind(win, off), r[0], ALU.min), [win, off, r], [out])
+    def differ(t, h, a, b):
+        name, o = dy(t, h)
+        out, win = A(name, o + 16 * a, o + 16 * b), A("BW", 0, W + t * K)
+        off = A("PU", h * HC + a, h * HC + b) if t else lists("LU", 0, h, 0, a, b)
+        r = A("SW", site(t, h, 2) + 16 * a, site(t, h, 2) + 16 * b)
+        add("v", "c", lambda q: g.vector.tensor_tensor(out[0], ind(win, off), r[0], ALU.subtract), [win, off, r], [out],
+            US["v"] + out[2] * US["gather"], sort="gather")
+        ts(A("MM", mo(t, h) + 16 * a, mo(t, h) + 16 * b), out, A("EB", 0, 1), ALU.min, -2.0, ALU.mult)
+
+    def least(out, win, off, r, y):
+        if OPT["plain"]:
+            return tt(out, y, r, ALU.min)
+        add("v", "c", lambda q: g.vector.tensor_tensor(out[0], ind(win, off), r[0], ALU.min), [win, off, r], [out],
+            US["v"] + out[2] * US["gather"], sort="gather")
 
     def links(t, h):
+        if OPT["mode"][2 * t + h] == "y":
+            win, o = A("BW", 0, W + t * K), site(t, h, 0)
+            for a, b in pieces(GQ):
+                off = A("PU", h * HC + a, h * HC + b) if t else lists("LU", 0, h, 0, a, b)
+                tag[0] = ("visit", t, h)
+                gather(A("SW", o + 16 * a, o + 16 * b), win, off)
+                tag[0] = ("least", t, h)
+                least(A("MM", mo(t, h) + 16 * a, mo(t, h) + 16 * b), win, off,
+                      A("SW", site(t, h, 2) + 16 * a, site(t, h, 2) + 16 * b), A("SW", o + 16 * a, o + 16 * b))
+            tag[0] = ("links", t, h)
+            extract(pb(h, 0), RB, "MM", mo(t, h))
+            extract(pg(h, 0), RG, "MM", mo(t, h))
+            extract(pg(h, 3), RL, "SW", o)
+            if t < STEPS - 1:
+                records(t, h, 1)
+            return
+        for o, role in ((pb, RB), (pg, RG)):
+            extract(o(h, 0), role, "SW", site(t, h, 2), last=False, bank=A(o(h, 0)[1][0]))
         for a, b in pieces(GQ):
-            gather(A("RW", reg(t, h, 2) + 16 * a, reg(t, h, 2) + 16 * b), A("BW", 0, W + t * K),
-                   A("PU" if t else "LU", h * HC + a, h * HC + b))
-            least(t, h, a, b)
-        extract(half("P6", h), RB, "MM", mo(t, h))
-        extract(half("P7", h), RBL, "MM", mo(t, h))
-        extract(half("P7", h, C), RL, "RW", reg(t, h, 2))
+            differ(t, h, a, b)
+        for o, role in ((pb, MB), (pg, MG)):
+            extract(o(h, 0), role, "MM", mo(t, h), first=False, bank=A(o(h, 0)[1][0]))
+        if t < STEPS - 1 and OPT["fold"]:
+            records(t, h, 1)
+        accumulate(block("SW", site(t, h, 0)), block("DY", h * H) if aside(t, h) else block("SW", site(t, h, 2)))
+        if t < STEPS - 1 and not OPT["fold"]:
+            records(t, h, 1)
 
     def hold(t, h):
-        act(half("BD", h), half("P6", h), AF.Sign)
-        act(half("NB", h), half("P6", h), AF.Relu, bias=BIG, scale=-BIG)
-        act(half("G1", h), half("P7", h), AF.Relu)
-        mm([[(half("P3", h), A("BO"), half("BD", h))],
-            [(half("P3", h, C), A("DF", 0, 128), half("FL", h, t * C)), (half("P3", h, C), db(IDB), half("NB", h))]])
-        tt(half("WW", h), half("P6", h), half("G1", h), ALU.subtract)
-        tt(half("FB", h), half("P3", h), half("WW", h), ALU.mult)
-        tt(half("NH", h), half("P3", h, C), half("FB", h), ALU.is_gt)
-        tt(half("LE", h), half("P7", h, C), half("WW", h), ALU.subtract)
+        tag[0] = ("hold", t, h)
+        act(half("BD", h), pb(h, 0), AF.Sign)
+        act(half("G1", h), pg(h, 0), AF.Relu, scale=1.0 - 2.0 ** -18)
+        mm([[(pb(h, 1), A("BO"), half("BD", h))]])
+        tt(half("WW", h), pb(h, 0), half("G1", h), ALU.subtract)
+        tt(pb(h, 1), pb(h, 1), half("WW", h), ALU.mult)
+        tt(nh(t, h), pb(h, 1), half("FL", h, t * C), ALU.is_lt)
         act(half("GT", h), half("G1", h), AF.Sign)
-        act(half("SG", h), half("LE", h), AF.Sign, bias=0.5, scale=-1.0)
+        if OPT["mode"][2 * t + h] == "y":
+            return tt(half("EE", h), pg(h, 3), half("WW", h), ALU.is_gt)
+        copy(half("RI", h), pg(h, 0))
+        tt(half("EE", h), half("RI", h), pg(h, 0), ALU.subtract)
 
     def move(t, h):
         c = h * HC
-        tt(half("UU", h), half("NH", h), half("DDF", h), ALU.mult)
+        tag[0] = ("free", t, h)
         for a, b in pieces(GQ):
             gather(A("X4", 16 * (c + a), 16 * (c + b)), A("OW"), A("DU", c + a, c + b), empty=True)
-        extract(half("P5", h, C), RC + t, "X4", h * H)
-        tt(half("UU", h), half("P5", h, C), half("UU", h), ALU.mult)
-        if h:
-            s, o = 128 - SH, half("P4", 1, C)
-            mm([[(o, A("DF", s, s + 128), half("LF", 1)), (o, A("DF", s, s + 128), half("UU", 1))]])
-        else:
-            o = half("UU", 0)
-            tt(o, o, half("LF", 0), ALU.add)
-        copy(half("NP", h, t * C), o)
-        send(1, half("LU", h, (t + 1) * C), half("NP", h, t * C), "a%s%d" % ("nm"[h], t + 1), True)
+        tag[0] = ("names", t, h)
+        tt(half("UU", h), nh(t, h), half("DDF", h), ALU.mult)
+        extract(half("P7", h), RC + t, "X4", h * H)
+        tt(half("UU", h), half("P7", h), half("UU", h), ALU.mult)
+        if not h:
+            tt(lists("MO", t, 0), half("UU", 0), names(t, 0), ALU.add)
+            send(1, lists("LF", t + 1, 0), lists("MO", t, 0), "an%d" % (t + 1), True)
 
     def swap(t, h):
+        tag[0] = ("again", t, h)
         if not h:
             for a, b in pieces(GQ):
-                gather(A("XC", 16 * a, 16 * b), A("OW"), A("LU", t * C + a, t * C + b))
-        o = half("P5", h)
-        extract(o, RC + t, "XG" if h else "XC", h * H, [(o, db(NEG), half("GT", h)), (o, db(NEG), half("NH", h))])
-        act(half("SW", h), o, AF.Relu, scale=-1.0)
-        tt(half("AL", h), half("SW", h), half("SG", h), ALU.mult)
-        o = half("P6", h, C)
-        mm([[(o, A("DF", 0, 128), A("CJ")), (o, db(WIDE), half("AL", h))]])
-        copy(half("IU", h), o)
-        o, u = mo(t + 1, h), W + t * K + h * H
-        for j, (a, b) in enumerate(pieces(2)):
-            gather(A("RS", o + 16 * a, o + 16 * b), A("RW", reg(t, h, 0), reg(t, h, 3)), A("IU", h * HC + a, h * HC + b))
-            if t < STEPS - 1:
-                records(t + 1, h, j)
-        for a, b in pieces(GQ):
-            gather(A("BW", u + 16 * a, u + 16 * b), A("RW", reg(t, h, 1), reg(t, h, 4)), A("IU", h * HC + a, h * HC + b))
-
-    def halve(x, n):
-        out, in_ = A("XE", x, x + n), A("XE", x + n, x + 2 * n)
-        add("g", "d", lambda q: g.dma_start(out[0], in_[0], accum_op=ALU.add), [in_, out], [out])
+                gather(A("XC", 16 * a, 16 * b), A("OW"), lists("LU", t, 0, 0, a, b))
+        tag[0] = ("list", t, h)
+        o = pg(h, 1)
+        extract(o, RC + t, "XG" if h else "XC", h * H,
+                [(o, db(NEG), half("GT", h)), (o, db(FLAG), half("EE", h)), (o, db(NEG), nh(t, h))])
+        act(half("VV", h), o, AF.Relu, bias=-1.0, scale=-2.0)
+        o, iu = pg(h, 2), half("IU", h, t * C)
+        mm([[(o, db(IDB), A("CB")), (o, db(WIDE), half("VV", h))]])
+        ts(iu, o, col(KCOL), ALU.add)
+        if t < STEPS - 1 and h:
+            s, o, u = 128 - SH, half("P7", 0, C), half("P7", 1, C)
+            mm([[(o, A("DF", s, s + 128), lists("LF", t, 1)), (o, A("DF", s, s + 128), half("UU", 1))],
+                [(u, A("DF", 0, 128), A("CJ")), (u, db(BACK + s), half("VV", 1))]])
+            evac(lists("MO", t, 1, 0, 0, C), A("P7", C, 2 * C))
+            send(1, lists("LF", t + 1, 1, 0, 0, C), lists("MO", t, 1, 0, 0, C), "am%d" % (t + 1), True)
+        elif t < STEPS - 1:
+            send(1, lists("LU", t + 1, 0, 1), iu, "ai%d" % (t + 1), True)
+        for name, u, j in ((("RS", h * H, -1),) if t == STEPS - 1 else ()) + (("BW", W + t * K + h * H, 0),):
+            tag[0] = ("own" if j else "site", t, h)
+            for a, b in pieces(GQ):
+                gather(A(name, u + 16 * a, u + 16 * b), A("SW", site(t, h, j), site(t, h, j + 3)),
+                       A("IU", t * C + h * HC + a, t * C + h * HC + b))
 
     def totals(t, h):
-        s, x = (SH * (t + 1) * h) % 128, mo(t, h)
-        tail = t == STEPS - 1 and h
+        s, x, e = (SH * (t + 1) * h) % 128, mo(t, h), h * H
+        tail = 2 * t + h >= 2 * STEPS - OPT["tail"]
+        acc = A("P6" if tail and h else "P7", 2 * C, 2 * C + HC)
+        mode = OPT["mode"][2 * t + h]
+        tag[0] = ("totals", t, h)
+        terms = {"a": [], "y": [(IDB, "SW", site(t, h, 2)), (IDB, "SW", site(t, h, 0))], "d": [(IDB, "DY", h * H)], "g": [(NEG, "SW", site(t, h, 2)), (IDB, "SW", site(t, h, 0))]}[mode]
+        if mode == "a":
+            accumulate(block("MM", x), block("DY", h * H))
         for i in range(4):
             bank, grps = "P%d" % (i % 2), []
             for kk in range(4):
                 k = 4 * i + kk
                 o = A(bank, kk * HC, (kk + 1) * HC)
-                grps.append([(o, db(IDB), A("RW", reg(t, h, 2) + k, reg(t, h, 3), 16)),
-                             (o, db(IDB), A("RW", reg(t, h, 1) + k, reg(t, h, 2), 16)),
-                             (o, db(NTWO), A("MM", mo(t, h) + k, mo(t, h) + H, 16)),
-                             (o, A("MK", k * 128, (k + 1) * 128), half("NH", h))])
+                grps.append([(o, db(NTWO if mode == "y" else IDB), A("MM", x + k, x + H, 16))]
+                            + [(o, db(m), A(name, u + k, u + H, 16)) for m, name, u in terms]
+                            + [(o, A("MK", k * 128, (k + 1) * 128), nh(t, h))])
             mm(grps)
-            act(A("XE", x + i * 2 * C, x + (i + 1) * 2 * C), A(bank, 0, 2 * C), AF.Exp, scale=-1.0 / 64)
+            act(A("XE", e + i * 2 * C, e + (i + 1) * 2 * C), A(bank, 0, 2 * C), AF.Exp, scale=-1.0 / 64)
             if tail:
-                mm([[(half("P4", h), A("DF", s, s + 128), half("XE", 0, x + k * HC)) for k in range(4 * i, 4 * i + 4)]],
-                   i == 0, i == 3, A("P4"))
+                mm([[(acc, A("DF", s, s + 128), half("XE", 0, e + k * HC)) for k in range(4 * i, 4 * i + 4)]],
+                   i == 0, i == 3, A(acc[1][0]))
         if not tail:
-            halve(x, 8 * HC)
-            halve(x, 4 * HC)
-            mm([[(half("P2", h), A("DF", s, s + 128), half("XE", 0, x + k * HC)) for k in range(4)]])
-        evac(half("ES", h, t * C), half("P4" if tail else "P2", h))
+            for n in (8 * HC, 4 * HC)[:OPT["halve"]]:
+                accumulate(A("XE", e, e + n), A("XE", e + n, e + 2 * n))
+            mm([[(acc, A("DF", s, s + 128), half("XE", 0, e + k * HC)) for k in range(16 >> OPT["halve"])]])
+        evac(half("ES", h, t * C), acc)
         if h:
             send(-(t + 1), A("EL", t * C, (t + 1) * C), A("ES", t * C, (t + 1) * C), "ae%d" % t, True)
 
+    def latest(t):
+        tag[0] = ("latest", t, 0)
+        for j in range(2):
+            dma("y", A("DD", j * 256, (j + 1) * 256), A("OW", p=(2 + 3 * t + j, 128, 16)))
+        o = A("P2", 256, 512)
+        mm([[(o, db(IDB), A("DD", 0, 256)), (o, db(HIGH), A("DD", 256, 512))]])
+        if t < STEPS - 1:
+            evac(A("PF", 0, 256), o)
+        else:
+            tt(A("PF", 256, 512), o, A("PF", 0, 256), ALU.max)
+            copy(A("PFU"), A("PF", 256, 512))
+
     for t in range(STEPS):
-        for j in range(2 if t else 0):
-            o, u, n = reg(t, 1, 1) + j * H // 2, (t - 1) * H + j * H // 2, H // 2
-            dma("y", A("RW", o, o + n, p=(SH, 128)), A("STG", u, u + n, p=(0, 128 - SH)))
-            dma("y", A("RW", o, o + n, p=(0, SH)), A("STG", u, u + n, p=(128 - SH, 128)))
         for h in range(2):
-            if t == 0:
-                copy(half("LU", h), half("NL", h))
-            copy(half("LF", h), half("LU", h, t * C) if t else half("NL", h))
+            receptors(t, h)
             board(t, h)
             links(t, h)
             hold(t, h)
+        tag[0] = None
+        for j in range(2 if t < STEPS - 1 else 0):
+            dma("y", A("CC", p=(2 + 3 * t + j, 128, 16)), A("SW", site(0, 0, 1), site(0, 0, 1) + 384, p=(0, 64)))
+            if t:
+                dma("y", A("CC", p=(5 + 3 * t + j, 128, 16)), A("JD", 384 * j, 384 * (j + 1), p=(0, 64)))
         for h in range(2):
             if t < STEPS - 1:
                 move(t, h)
             swap(t, h)
+        if t:
+            latest(t)
+        for h in range(2):
             totals(t, h)
-        for j in range(2):
-            c = j * 128
-            extract(A("P2", 256 + c, 384 + c), RZ + t, "OW", 16 * c)
-            tt(A("PF", c, c + 128), A("P2", 256 + c, 384 + c), A("PF" if t else "SF", c, c + 128), ALU.max)
 
-    copy(A("PFU"), A("PF"))
-    s, b = (SH * STEPS) % 128, mo(STEPS, 0)
+    s = (SH * STEPS) % 128
+    tag[0] = ("home", STEPS - 1, 0)
     for j in range(2):
-        o, c = A("P%d" % (6 + j), 0, 384), b + j * 384
+        o, c = A("P%d" % (2 + j), 0, 384), j * 384
         mm([[(o, db(IDB), A("RS", c, c + 384)), (o, db(NEG), A("RS", c + 768, c + 768 + 384)),
              (o, db(TWO + s), A("RS", c + H, c + H + 384)), (o, db(NTWO + s), A("RS", c + H + 768, c + H + 768 + 384))]])
         evac(A("YS", j * 384, (j + 1) * 384), o)
         send(-STEPS, A("YL", j * 384, (j + 1) * 384), A("YS", j * 384, (j + 1) * 384), "ayr%d" % j, False)
         dma("y", T.yr[:, j * 384:(j + 1) * 384], A("YL", j * 384, (j + 1) * 384))
+    tag[0] = ("wall", STEPS - 1, 0)
+    for j in range(4):
+        c = j * 1024
+        gather(A("LW", c, c + 1024), A("BW"), A("PFU", j * 64, (j + 1) * 64))
+        mm([[(A("P%d" % (4 + k // 2), (k % 2) * 256 + j * 64, (k % 2) * 256 + (j + 1) * 64), db(m),
+              A("LW", c + 4 * u + k, c + 1024, 16)) for u, m in enumerate((IDB, NEG, TWO, NTWO))] for k in range(4)])
     for j in range(2):
-        for u in range(4):
-            c = u * 1024 + j * 512
-            gather(A("CC", c, c + 512), A("BW"), A("PFU", c // 16, c // 16 + 32))
-        o = A("P%d" % (3 + 2 * j))
-        mm([[(o, db(m), A("CC", u * 1024 + j * 512, u * 1024 + j * 512 + 512))
-             for u, m in enumerate((IDB, NEG, TWO, NTWO))]])
-        evac(A("YW", j * 512, (j + 1) * 512), o)
-        dma("y", T.yw[:, j * 512:(j + 1) * 512], A("YW", j * 512, (j + 1) * 512))
-    tt(A("EL", 3 * C, 4 * C), A("EL", 0, C), A("EL", C, 2 * C), ALU.add)
-    tt(A("EL", 3 * C, 4 * C), A("EL", 3 * C, 4 * C), A("EL", 2 * C, 3 * C), ALU.add)
+        evac(A("YW", j * 512, (j + 1) * 512), A("P%d" % (4 + j)))
+        dma("ys"[j], T.yw[:, j * 512:(j + 1) * 512], A("YW", j * 512, (j + 1) * 512))
+    tag[0] = ("sum", STEPS - 1, 0)
+    accumulate(A("EL", 0, C), A("EL", C, 2 * C))
+    tt(A("EL", 3 * C, 4 * C), A("EL", 0, C), A("EL", 2 * C, 3 * C), ALU.add)
     dma("y", T.ye[:], A("EL", 3 * C, 4 * C))
     _emit(g, T, ops)

from concourse.bass import DstId, RemoteDMATransfer
from concourse.mybir import AluOpType as ALU
from concourse.mybir import ActivationFunctionType as AF

W, C, K, H = 4096, 192, 3072, 1536
HC = C // 2
STEPS = 3
SH = 48
RZ, RD, RC, RB, RG, MB, MG = 0, 3, 4, 7, 8, 9, 10
NROLE = 11
RL = 9
GQ, SQ = 2, 3
EPS = 2.0 ** -13
US = {"plain": 0.0009, "gather": 0.0012, "scatter": 0.0026, "pe": 0.00046, "v": 0.07, "s": 0.1, "wake": 0.12,
      "dma": 1.8, "gdma": 0.9, "remote": 0.6, "hop": 1.9, "first": 2.8, "margin": 0.5, "local": 1 / 540e3,
      "near": 1 / 330e3, "far": 1 / 160e3}
OPT = {"mode": "yyyyyy", "fold": 0, "via": 2, "halve": 1, "plain": 1, "lean": 0.5, "tries": 45000, "seed": 3, "heat": 1.5,
       "tail": 1}
CASES = ({"plain": 1.0, "lag": 1.0, "us": 95}, {"scatter": 1.8, "gather": 1.4, "plain": 1.2, "lag": 1.1, "us": 130},
         {"scatter": 0.7, "gather": 0.8, "plain": 0.95, "lag": 1.25, "us": 95})

bf, f32, i32, u16 = "bfloat16", "float32", "int32", "uint16"
SCRATCH = {
    "BW": ("sbuf", [128, W + 3 * K], bf), "OW": ("sbuf", [128, W], bf), "CC": ("sbuf", [128, K], bf),
    "SW": ("sbuf", [128, 14 * H], bf), "LW": ("sbuf", [128, 10 * H], bf), "XG": ("sbuf", [128, K], bf),
    "DY": ("sbuf", [128, K], bf), "XC": ("sbuf", [128, H], bf), "X4": ("sbuf", [128, K], bf),
    "MM": ("sbuf", [128, 2 * K], bf), "RS": ("sbuf", [128, K], bf), "XE": ("sbuf", [128, K], f32),
    "MK": ("sbuf", [128, 2048], bf), "WR": ("sbuf", [128, NROLE * 144], bf), "DF": ("sbuf", [128, 256], f32),
    "DB": ("sbuf", [128, 1408], bf), "SEL": ("sbuf", [128, 256], f32), "BO": ("sbuf", [128, 128], bf),
    "JD": ("sbuf", [128, 768], bf), "NI": ("sbuf", [128, C], i32), "NL": ("sbuf", [128, C], i32),
    "LU": ("sbuf", [128, 6 * C], u16), "LF": ("sbuf", [128, 6 * C], f32), "MO": ("sbuf", [128, 4 * C], f32),
    "PU": ("sbuf", [128, C], u16), "DU": ("sbuf", [128, C], u16), "IU": ("sbuf", [128, 3 * C], u16),
    "PFU": ("sbuf", [128, 256], u16), "DI": ("sbuf", [128, 1536], i32), "DD": ("sbuf", [128, 1024], bf),
    "PLI": ("sbuf", [128, C], i32), "PLF": ("sbuf", [128, C], f32), "FS": ("sbuf", [128, 3 * C], f32),
    "FL": ("sbuf", [128, 3 * C], f32), "EI": ("sbuf", [128, 64], i32), "EF": ("sbuf", [128, 80], f32),
    "EB": ("sbuf", [128, 8], bf), "CJ": ("sbuf", [128, HC], f32), "CB": ("sbuf", [128, HC], bf), "PF": ("sbuf", [128, 512], f32),
    "DDF": ("sbuf", [128, C], f32), "G1": ("sbuf", [128, C], f32), "WW": ("sbuf", [128, C], f32),
    "UU": ("sbuf", [128, C], f32), "RI": ("sbuf", [128, C], i32),
    "GT": ("sbuf", [128, C], bf), "EE": ("sbuf", [128, C], bf), "VV": ("sbuf", [128, C], bf),
    "BD": ("sbuf", [128, C], bf), "NH": ("sbuf", [128, 2 * C], bf),
    "ES": ("sbuf", [128, 3 * C], f32), "EL": ("sbuf", [128, 4 * C], f32),
    "YS": ("sbuf", [128, 768], f32), "YL": ("sbuf", [128, 768], f32), "YW": ("sbuf", [128, 1024], f32),
}
for _b in range(8):
    SCRATCH["P%d" % _b] = ("psum", [128, 512], f32)
SEMAPHORES = (["cv", "cs", "ct", "cg", "sent", "outs", "ayr0", "ayr1"] + ["d%d" % _i for _i in range(90)]
              + ["a%s%d" % (_k, _t) for _k in "nmiabcdfe" for _t in range(3)]
              + ["h%d" % _i for _i in range(4)] + ["k%d" % _i for _i in range(4)])
COUNTER = {"v": "cv", "s": "cs", "t": "ct", "g": "cg"}
SIZE = {bf: 2, u16: 2, f32: 4, i32: 4}
PLAN = {}


def _clash(a, b):
    return a[0] == b[0] and a[1] < b[2] and b[1] < a[2] and bool(a[3] & b[3])


def _hit(o, p):
    if not (o["names"] & p["names"]):
        return False
    return (any(_clash(a, b) for a in o["w"] for b in p["r"] + p["w"])
            or any(_clash(a, b) for a in o["r"] for b in p["w"]))


def _order(ops, deps):
    n = len(ops)
    sender = {op["sem"]: i for i, op in enumerate(ops) if op["kind"] == "r"}
    pre = [set(deps[i]) | ({sender[op["sem"]]} if op["kind"] == "a" else set()) for i, op in enumerate(ops)]
    post = [[] for _ in ops]
    for i in range(n):
        if "behind" in ops[i]:
            pre[i].add(ops[i]["behind"])
        for m in pre[i]:
            post[m].append(i)
    wake = US["wake"]

    hold, lag = [op["hold"] for op in ops], [op["lag"] for op in ops]
    use, banks = [op.get("use", 0.0) for op in ops], [sorted(op["ps"]) for op in ops]
    soft = [op.get("behind") for op in ops]
    pre = [sorted(x) for x in pre]

    def gap(spans, t, d, q=None):
        lo, hi = 0, len(spans)
        while lo < hi:
            mid = (lo + hi) // 2
            if spans[mid][0] < t - 4.0:
                lo = mid + 1
            else:
                hi = mid
        for a, b, r in spans[lo:]:
            if a >= t + d:
                break
            if b > t and r != q:
                t = b
        return t

    def book(spans, x):
        spans.append(x)
        if len(spans) > 1 and spans[-2] > x:
            spans.sort()

    def sweep(turn, side):
        busy = {x: [] for x in list("vstgyL") + ["P%d" % b for b in range(8)]}
        queue, start, done = [None] * n, [0.0] * n, [0.0] * n
        for i in turn:
            est = 0.0
            for m in pre[i]:
                t = start[m] + hold[m] if soft[i] == m else done[m] + wake
                if t > est:
                    est = t
            q = ops[i]["q"]
            if q is None:
                start[i], done[i] = est, est + lag[i]
                continue
            pick = None
            for q in side[i] if q == "x" else q:
                t, lead = est, hold[i] + lag[i] - use[i] - 1.0
                while True:
                    u = gap(busy[q], t, hold[i])
                    for x in banks[i]:
                        u = gap(busy[x], u, hold[i], q)
                    if use[i]:
                        u = gap(busy["L"], u + lead, use[i]) - lead
                    if u <= t + 1e-9:
                        break
                    t = u
                if pick is None or t + OPT["lean"] < pick[0]:
                    pick = (t, q)
            t, q = pick
            queue[i], start[i], done[i] = q, t, t + hold[i] + lag[i]
            book(busy[q], (t, t + hold[i], ""))
            for x in banks[i]:
                book(busy[x], (t - wake, t + hold[i] + wake, q))
            if use[i]:
                book(busy["L"], (t + lead, t + lead + use[i], ""))
        return queue, start, done

    def replay(order, queue, k):
        hold, lag, use = k
        last, bank, done, end, why = {}, {}, [0.0] * n, [0.0] * n, [None] * n
        line = (0.0, None)
        for i in order:
            q, t = queue[i], 0.0
            if q in last:
                why[i] = last[q]
                t = end[why[i]]
            for m in hard[i]:
                if done[m] + wake > t:
                    t, why[i] = done[m] + wake, m
            for x in banks[i]:
                m = bank.get(x)
                if m is not None and queue[m] != q and end[m] + wake > t:
                    t, why[i] = end[m] + wake, m
                bank[x] = i
            end[i] = t = t + hold[i]
            if q is not None:
                last[q] = i
            done[i] = t = t + lag[i]
            if use[i]:
                if line[0] + use[i] + 1.0 > t:
                    done[i], why[i] = line[0] + use[i] + 1.0, line[1]
                line = (done[i] - 1.0, i)
        PLAN["why"] = (why, done, end)
        i, chain = done.index(max(done)), []
        while why[i] is not None:
            if why[i] not in hard[i]:
                chain.append((i, why[i]))
            i = why[i]
        return max(done), chain, end

    hard, above = [[m for m in pre[i] if soft[i] != m] for i in range(n)], [0] * n
    for i in _topological(pre, post):
        implied = 0
        for m in hard[i]:
            implied |= above[m]
        for m in hard[i]:
            above[i] |= above[m] | 1 << m
        hard[i] = [m for m in hard[i] if not implied >> m & 1]
    cases = [([hold[i] * k.get(ops[i].get("sort"), k["plain"]) for i in range(n)], [x * k["lag"] for x in lag],
              [x * k["lag"] for x in use]) for k in CASES]

    def judge(key, side):
        queue, start, done = sweep(sorted(range(n), key=lambda i: key[i]), side)
        return weigh(sorted(range(n), key=lambda i: (start[i], done[i])), queue)

    def weigh(order, queue):
        runs = [replay(order, queue, k) for k in cases]
        return (sum(r[0] / k["us"] * 100 + sum(r[2]) / n / 30 for r, k in zip(runs, CASES)), [r[0] for r in runs],
                order, queue, [x for r in runs for x in r[1]], [a - b for a, b in zip(runs[0][2], cases[0][0])])

    way = [0.0] * n
    for i in reversed(_topological(pre, post)):
        way[i] = hold[i] + lag[i] + wake + max([0.0] + [way[m] for m in post[i]])
    side = ["sv"] * n
    best = now = judge([-x for x in way], side)
    free = [i for i in range(n) if ops[i]["q"] == "x"]
    seed = [OPT["seed"]]

    def draw(k):
        seed[0] = (seed[0] * 1103515245 + 12345) % 2 ** 31
        return (seed[0] >> 8) % k

    def shift(order, i, to):
        at = order.index(i)
        near, part = (pre, order[to:at + 1]) if to < at else (post, order[at:to + 1])
        on, take, todo = set(part), {i}, [i]
        for m in todo:
            for x in near[m]:
                if x in on and x not in take:
                    take.add(x)
                    todo.append(x)
        a, b = [x for x in part if x in take], [x for x in part if x not in take]
        return order[:to] + a + b + order[at + 1:] if to < at else order[:at] + b + a + order[to + 1:]

    if "start" in OPT:
        best = now = weigh([abs(x) - 1 for x in OPT["start"]], [
            ("v" if -(i + 1) in OPT["start"] else "s") if ops[i]["q"] == "x" else ops[i]["q"] for i in range(n)])
    for it in range(OPT["tries"]):
        order, queue = now[2], now[3]
        i, p = now[4][draw(len(now[4]))]
        how = draw(10)
        if how < 3:
            i = (i, p, free[draw(len(free))])[how]
            if ops[i]["q"] != "x":
                continue
            queue = list(queue)
            queue[i] = "s" if queue[i] == "v" else "v"
            if draw(2):
                order = shift(order, i, max(0, min(n - 1, order.index(i) + draw(41) - 20)))
        elif how < 6:
            order = shift(order, i, max(0, order.index(p) - (0, 0, 5, 20)[draw(4)]))
        elif how < 9:
            order = shift(order, p, min(n - 1, order.index(i) + (0, 0, 5, 20, 60)[draw(5)]))
        else:
            i = draw(n)
            order = shift(order, i, max(0, min(n - 1, order.index(i) + draw(61) - 30)))
        new = weigh(order, queue)
        if new[0] <= now[0] + OPT["heat"] * (1 - it / OPT["tries"]) * draw(100) / 100:
            if it % 8 == 0:
                new = min(new, weigh(sorted(order, key=lambda m: new[5][m]), queue), key=lambda r: r[0])
            now = new
            if new[0] < best[0]:
                best = new
    PLAN["us"] = best[1]
    PLAN["code"] = [-(i + 1) if best[3][i] == "v" and ops[i]["q"] == "x" else i + 1 for i in best[2]]
    replay(best[2], best[3], cases[OPT.get("show", 0)])
    PLAN["ops"] = (ops, best[3], hard)
    return best[2], best[3]


def _topological(pre, post):
    left = [len(x) for x in pre]
    turn = [i for i in range(len(pre)) if not left[i]]
    for i in turn:
        for m in post[i]:
            left[m] -= 1
            if not left[m]:
                turn.append(m)
    return turn


def _plan(ops):
    deps = [{m for m in range(i) if _hit(ops[m], op)} for i, op in enumerate(ops)]
    order, queue = _order(ops, deps)
    known = {q: set() for q in "vstgy"}
    before = {q: set() for q in "vstgy"}
    seen, waits, need = {}, {}, set()
    for x, i in enumerate(order):
        op, q = ops[i], queue[i]
        if q is None:
            seen[i] = {i}
            continue
        ds = deps[i] | {m for m in order[:x] if queue[m] != q and ops[m]["ps"] & op["ps"]}
        waits[i] = []
        for m in reversed(order[:x]):
            if m in ds and m not in known[q] and not (q == "t" and queue[m] == "t"):
                waits[i].append(m)
                need.add(m)
                known[q] |= seen[m]
        seen[i] = set(known[q]) | {i}
        if op["kind"] == "c":
            seen[i] |= before[q]
            before[q].add(i)
    return order, queue, waits, need


def _emit(g, T, ops):
    if "plan" not in PLAN:
        PLAN["plan"] = _plan(ops)
    order, queue, waits, need = PLAN["plan"]
    eng = {"v": g.vector, "s": g.scalar, "t": g.tensor, "g": g, "y": g.sync}
    count = {q: 0 for q in COUNTER}
    nd, total = 0, {"sent": 0, "outs": 0}
    for i in order:
        op, q = ops[i], queue[i]
        if q is None:
            continue
        for m in waits[i]:
            s, v = ops[m]["tok"]
            eng[q].wait_ge(T.sem[s], v)
        if op["kind"] == "c":
            call = op["fn"](q)
            if i in need:
                count[q] += 1
                call.then_inc(T.sem[COUNTER[q]], 1)
                op["tok"] = (COUNTER[q], count[q])
            continue
        n = 16 if op["kind"] == "d" else op["n"]
        if i in need:
            s = "d%d" % nd
            nd += 1
            op["tok"] = (s, n)
        else:
            s = "outs" if op["kind"] == "d" else "sent"
            total[s] += n
        if op["kind"] == "d":
            op["fn"](q).then_inc(T.sem[s], 16)
        else:
            op["fn"](T.sem[s])
    g.wait_ge(T.sem["sent"], total["sent"])
    g.sync.wait_ge(T.sem["outs"], total["outs"])


def _carrier(T, topo, rank, h):
    core, nxt = T.cores[rank], T.cores[(rank + 1) % len(T.cores)]
    if h == 0 and topo.chip(core) == topo.chip(nxt):
        return None
    return [c for c in topo.cores_of(core)
            if T.rank_of(c) is None and topo.die(c) != topo.die(core) and topo.may_write(c, nxt)][h]


def _window(t, h, j):
    return (5 * (t - 1) + (4 - j if h else j)) * H


def _hand_on(g, core, T, topo, rank, h):
    dst = T.cores[(rank + 1) % len(T.cores)]
    rid, pid, _ = topo.addr(dst)
    n = len(topo.engines(T.cores[rank], core))
    blocks = [b for b in range(4) if h or b % 2 < OPT["via"]]
    for b in blocks:
        a, o = b * H, (4 + b) * H
        if h:
            for q, to, fro in ((g.sync, slice(SH, 128), slice(0, 128 - SH)), (g.scalar, slice(0, SH), slice(128 - SH, 128))):
                q.wait_ge(T.sem["h%d" % b], n)
                q.dma_start(T.LW[to, o:o + H], T.LW[fro, a:a + H]).then_inc(T.sem["k%d" % b], 16)
            g.wait_ge(T.sem["k%d" % b], 32)
            a = o
        else:
            g.wait_ge(T.sem["h%d" % b], n)
        t, j = 1 + b // 2, b % 2
        u = _window(t, h, j)
        g.remote_dma(T.LW[:, u:u + H], T.LW[:, a:a + H], T.sem["a%s%d" % ("abcd"[2 * h + j], t)], T.sem["sent"],
                     pid, rid, topo.mask(core, dst))
    if blocks:
        g.wait_ge(T.sem["sent"], len(blocks) * len(topo.engines(core, dst)))


def rank_program(g, core, T, topo):
    rank = T.rank_of(core)
    N = len(T.cores)
    if rank is None:
        for r in range(N):
            for h in range(2):
                if _carrier(T, topo, r, h) == core:
                    _hand_on(g, core, T, topo, r, h)
        return
    ops, tag = [], [None]
    ALLP = frozenset(range(128))

    def A(name, c0=None, c1=None, step=1, p=None):
        t = T[name]
        c0 = 0 if c0 is None else c0
        c1 = t.shape[1] if c1 is None else c1
        ps = slice(0, 128) if p is None else slice(*p)
        cs = slice(c0, c1) if step == 1 else slice(c0, c1, step)
        return (t[ps, cs], (name, c0, c1, ALLP if p is None else frozenset(range(128)[ps])), len(range(c0, c1, step)))

    def add(q, kind, fn, r, w, hold, lag=0.0, **kw):
        r = [x[1] for x in r if isinstance(x, tuple)]
        w = [x[1] for x in w]
        op = {"q": q, "kind": kind, "fn": fn, "r": r, "w": w, "names": frozenset(x[0] for x in r + w),
              "ps": frozenset(x[0] for x in r + w if SCRATCH[x[0]][0] == "psum"), "hold": hold, "lag": lag,
              "tag": tag[0]}
        op.update(kw)
        ops.append(op)

    def val(x):
        return x[0] if isinstance(x, tuple) else x

    def ind(win, off):
        return win[0].indirect(off[0])

    def size(x):
        return SIZE[SCRATCH[x[1][0]][2]]

    def plain(q, xs, k=1.0):
        if q == "v" and all(size(x) == 2 for x in xs):
            k /= 2
        return US[q] + max(64, xs[0][2] * k) * US["plain"]

    def copy(out, in_):
        add("v", "c", lambda q: g.vector.tensor_copy(out[0], in_[0]), [in_], [out], plain("v", [out, in_]))

    def tt(out, a, b, op):
        k = 2.0 if all(SCRATCH[x[1][0]][0] == "sbuf" for x in (a, b)) else 1.0
        add("v", "c", lambda q: g.vector.tensor_tensor(out[0], a[0], b[0], op), [a, b], [out], plain("v", [out, a, b], k))

    def ts(out, a, s1, op0, s2=None, op1=None):
        more = () if op1 is None else (op1,)
        add("v", "c", lambda q: g.vector.tensor_scalar(out[0], a[0], val(s1), val(s2), op0, *more), [a, s1, s2], [out],
            plain("v", [out, a]))

    def fill(out, c):
        add("v", "c", lambda q: g.vector.memset(out[0], c), [], [out], plain("v", [out]))

    def act(out, in_, func, bias=0.0, scale=1.0):
        add("s", "c", lambda q: g.scalar.activation(out[0], in_[0], func, bias=val(bias), scale=val(scale)),
            [in_, bias, scale], [out], plain("s", [out]))

    def evac(out, in_, mul=None):
        def fn(q):
            if q == "s":
                return g.scalar.activation(out[0], in_[0], AF.Copy, scale=1.0 if mul is None else mul[0])
            if mul is None:
                return g.vector.tensor_copy(out[0], in_[0])
            return g.vector.tensor_scalar(out[0], in_[0], mul[0], None, ALU.mult)
        add("x", "c", fn, [in_, mul], [out], plain("s", [out]))

    def gather(out, win, off, mul=None, plus=None, empty=False):
        def fn(q):
            if q == "s":
                if empty:
                    return g.scalar.activation(out[0], ind(win, off), AF.Relu, bias=1.0, scale=-1.0)
                if mul is None:
                    return g.scalar.activation(out[0], ind(win, off), AF.Copy)
                return g.scalar.activation(out[0], ind(win, off), AF.Identity, bias=plus[0], scale=mul[0])
            if empty:
                return g.vector.tensor_scalar(out[0], ind(win, off), 0.0, None, ALU.is_equal)
            if mul is None:
                return g.vector.tensor_copy(out[0], ind(win, off))
            return g.vector.tensor_scalar(out[0], ind(win, off), mul[0], plus[0], ALU.mult, ALU.add)
        add("x", "c", fn, [win, off, mul, plus], [out], US["v"] + out[2] * US["gather"], sort="gather")

    def pieces(n):
        return [(HC * j // n, HC * (j + 1) // n) for j in range(n)]

    def mm(items, first=True, last=True, bank=None):
        def fn(q):
            r = None
            for grp in items:
                for n, (o, l, x) in enumerate(grp):
                    r = g.tensor.matmul(o[0], l[0], x[0], first and n == 0, last and n == len(grp) - 1)
            return r
        add("t", "c", fn, [y for grp in items for it in grp for y in it[1:]],
            [bank] if bank else [it[0] for grp in items for it in grp],
            sum(max(64, x[2]) * (4 if size(x) == 4 else 1) * US["pe"] for grp in items for _, _, x in grp), sort="pe")

    def extract(out, role, name, c0, more=(), **kw):
        mm([[(out, A("WR", role * 144 + 15 - k, role * 144 + 143 - k), A(name, c0 + k, c0 + 16 * out[2], 16))
             for k in range(16)] + list(more)], **kw)

    def iota(out, pattern, base, cm):
        kw = {} if SCRATCH[out[1][0]][2] == i32 else {"allow_small_or_imprecise_dtypes": True}
        add("g", "c", lambda q: g.iota(out[0], pattern, base, cm, **kw), [], [out], 0.13 + 2 * out[2] * US["plain"])

    def sel(buf, pattern, op, fillv, base, cm):
        add("g", "c", lambda q: g.affine_select(buf[0], buf[0], pattern, op, fillv, base, cm), [buf], [buf],
            0.17 + 2 * buf[2] * US["plain"])

    def span(x):
        return max(64, len(x[1][3])) * x[2] * size(x)

    def dma(q, out, in_, after=None):
        eng = g.sync if q == "y" else g.scalar
        sides = [x for x in (out, in_) if isinstance(x, tuple)]
        if min(len(x[1][3]) for x in sides) <= 8:
            kw = {"lag": US["dma"] + 0.6}
        else:
            use = 0.3 + span(sides[0]) * US["local"]
            kw = {"lag": US["dma"] + use, "on": "L", "use": use}
        add(q, "d", lambda q: eng.dma_start(val(out), val(in_)), [in_, after], [out] if isinstance(out, tuple) else [],
            0.06, **kw)

    def accumulate(out, in_):
        use = 0.3 + 2 * span(out) * US["local"]
        add("g", "d", lambda q: g.dma_start(out[0], in_[0], accum_op=ALU.add), [in_, out], [out], US["gdma"],
            US["dma"] + use + US["margin"], on="L", use=use)

    def engines(src, dst, small):
        e = topo.engines(src, dst)
        return e[::len(e) // 8] if small else e

    def write(dst, out, in_, sem, small, landing, on, plus=None):
        rid, pid, _ = topo.addr(dst)
        e = engines(core, dst, small)
        mask = sum(1 << x for x in e)
        use = (0.7 if on == "R" else 0.4) + span(in_) * (US["far" if on == "R" else "near"] + (US["local"] if plus else 0.0))

        def fn(ls):
            if plus is None:
                return g.remote_dma(out[0], in_[0], T.sem[sem], ls, pid, rid, mask)
            return g.remote_dma_fused([RemoteDMATransfer(
                dst_ids=[DstId(rid=rid, pnc=pid)], dma_engine_mask=mask, remote_sem=T.sem[sem],
                srcs=[in_[0], plus[0]], dsts=[out[0]], alu_op=1)], local_sem=ls)
        add("g", "r", fn, [in_, plus], [],
            US["remote"] + (US["first"] if landing == "an0" else 0.0), US["hop"] + use,
            n=len(e), sem=landing, on="L", use=use)

    def send(hop, out, in_, sem, small):
        write(T.cores[(rank + hop) % N], out, in_, sem, small, sem, "R")

    def arrive(src, out, sem, small, lag=0.0):
        add(None, "a", None, [], [out], 0.0, lag, sem=sem, tok=(sem, len(engines(src, core, small))))

    def behind(hop):
        return T.cores[(rank - hop) % N]

    def site(t, h, j):
        return (8 + 3 * h + j if t % 2 else 1 + 4 * h + j) * H

    def block(name, o):
        return A(name, o, o + H)

    def mo(t, h):
        return (t % 2) * K + h * H

    def half(name, h, base=0):
        return A(name, base + h * HC, base + (h + 1) * HC)

    def lists(name, t, h, j=0, a=0, b=HC):
        o = (2 * t + h) * C + j * HC
        return A(name, o + a, o + b)

    def records(t, h, j):
        tag[0] = ("pass" if j else "carry", t, h)
        via, sem = _carrier(T, topo, rank, h), "a%s%d" % ("abcd"[2 * h + j], t + 1)
        if j and OPT["fold"]:
            src, plus = block("SW", site(t, h, 2)), block(*dy(t, h))
        else:
            src, plus = block("SW", site(t, h, 2 - 2 * j)), None
        on = "L" if h or j < OPT["via"] else "R"
        if via is None or on == "R":
            write(behind(-1), block("LW", _window(t + 1, h, j)), src, sem, False, sem, on, plus)
        else:
            write(via, block("LW", (2 * t + j) * H), src, "h%d" % (2 * t + j), False, sem, on, plus)

    def wr(r0, n):
        return A("WR", r0 * 144 + 15, (r0 + n) * 144, 16)

    def db(j):
        return A("DB", j, j + 128)

    def col(j, n=1):
        return A("EF", j, j + n)

    IDB, NEG, BACK, TWO, NTWO, FLAG, HIGH, WIDE = 0, 128, 256, 512, 768, 1024, 1152, 1280
    MASKC, BIASC, G16, KCOL, LANE = 16, 20, 24, 26, 48

    for t in range(STEPS):
        for h in range(2):
            if t == 0:
                arrive(behind(1), half("NL", h), "a%s0" % "nm"[h], True)
                arrive(behind(1), block("SW", site(0, h, 2)), "a%s0" % "ac"[h], False)
                continue
            arrive(behind(1), lists("LF", t, h, 0, 0, (h + 1) * HC), "a%s%d" % ("nm"[h], t), True)
            via = _carrier(T, topo, (rank - 1) % N, h)
            for j in range(2):
                handed = h or j < OPT["via"]
                arrive(via if handed and via is not None else behind(1), block("LW", _window(t, h, j)),
                       "a%s%d" % ("abcd"[2 * h + j], t), False, (5.5 + 2.5 * h) * handed)
        if t:
            arrive(behind(1), lists("LU", t, 0, 1), "ai%d" % t, True)
        arrive(behind(t + 1), A("FL", t * C, (t + 1) * C), "af%d" % t, True)
        arrive(behind(-(t + 1)), A("EL", t * C, (t + 1) * C), "ae%d" % t, True)
    for j in range(2):
        arrive(behind(-STEPS), A("YL", j * 384, (j + 1) * 384), "ayr%d" % j, False)

    def in_turn(first):
        for i in range(first + 1, len(ops)):
            ops[i]["behind"] = i - 1

    first = len(ops)
    dma("y", A("NI", 0, HC), T.nm[:, 0:HC])
    dma("s", A("DI", 0, 256), T.dn[:])
    dma("y", A("NI", HC, C, p=(SH, 128)), T.nm[0:128 - SH, HC:C])
    dma("s", A("NI", HC, C, p=(0, SH)), T.nm[128 - SH:128, HC:C])
    dma("y", A("RS", 0, H), T.rc[:, 0:H])
    dma("s", A("PLI", p=(0, 8)), T.pl[:])
    dma("y", A("RS", H, K, p=(SH, 128)), T.rc[0:128 - SH, H:K])
    dma("y", A("RS", H, K, p=(0, SH)), T.rc[128 - SH:128, H:K])
    dma("y", A("BW", 0, W), T.wl[:])
    send(1, half("NL", 0), half("NI", 0), "an0", True)
    send(1, block("SW", site(0, 0, 2)), block("RS", 0), "aa0", False)
    send(1, half("NL", 1), half("NI", 1), "am0", True)
    send(1, block("SW", site(0, 1, 2)), block("RS", H), "ac0", False)
    in_turn(first)

    zero = block("SW", site(0, 0, 1))
    fill(zero, 0.0)
    fill(A("OW"), 0.0)
    iota(A("DI", 256, 512), [[1, 256]], 0, 256)
    ts(A("DI", 512, 1024), A("DI", 0, 512), 127, ALU.bitwise_and)
    ts(A("DI", 1024, 1536), A("DI", 0, 512), 7, ALU.logical_shift_right, 31, ALU.bitwise_and)
    copy(A("DD", 0, 512), A("DI", 512, 1024))
    copy(A("DD", 512, 1024), A("DI", 1024, 1536))
    for n, (row, j) in enumerate(((11, 0), (2, 1), (5, 1), (12, 2), (3, 3), (6, 3))):
        dma("sy"[n % 2], A("OW", p=(row, 128, 16)), A("DD", j * 256, (j + 1) * 256))
    iota(A("JD", 0, 384, p=(0, 64)), [[0, 3], [1, 128]], 0, 0)
    iota(A("JD", 384, 768, p=(0, 64)), [[1, 3], [0, 128]], 0, 3)
    fill(A("CC", 0, H), 0.0)
    fill(A("CC", H, K), 0.0)
    for n, row in enumerate((2, 3, 5, 6)):
        j = 384 * (n % 2)
        dma("sy"[n % 2], A("CC", 0, K, p=(row, 128, 16)), A("JD", j, j + 384, p=(0, 64)))
    iota(A("EI", 0, 16), [[-1, 16]], 16, 1)
    iota(A("EI", 32, 33), [[0, 1]], 0, 1)
    iota(col(28, 3), [[24, 3]], 32, 0)
    ts(A("EI", 16, 32), A("EI", 0, 16), 15, ALU.bitwise_and)
    ts(A("EI", 33, 34), A("EI", 32, 33), 4, ALU.logical_shift_right)
    ts(col(0, 16), A("EI", 16, 32), 0.0, ALU.is_equal)
    ts(col(25), A("EI", 33, 34), -24.0, ALU.mult)
    ts(col(G16), A("EI", 33, 34), -16.0, ALU.mult)
    tt(col(32, 3), A("EF", 2, 11, 3), A("EF", 3, 11, 3), ALU.add)
    ts(col(36, 3), col(28, 3), col(25), ALU.add)
    ts(col(MASKC, 3), col(32, 3), -1.0, ALU.mult, 1.0, ALU.add)
    tt(col(MASKC), col(MASKC), col(33), ALU.subtract)
    tt(col(40, 3), col(36, 3), A("EF", 3, 11, 3), ALU.mult)
    tt(col(BIASC, 3), col(40, 3), A("EF", 4, 11, 3), ALU.add)
    ts(col(BIASC), col(6), col(36), ALU.mult, col(BIASC), ALU.add)
    if "y" not in OPT["mode"]:
        ts(A("EB", 0, 1), col(15), EPS, ALU.mult)
    ts(col(LANE, 16), col(0, 16), 8192.0, ALU.mult)
    copy(col(KCOL), A("EI", 16, 17))
    act(A("WR", 0, MB * 144), A("SW", site(0, 0, 1), site(0, 0, 1) + MB * 144), AF.Copy)
    iota(wr(RZ, 4), [[-381, 4], [-2032, 9]], -253, 127)
    iota(wr(RC, 5), [[0, 45]], 1, 0)
    sel(wr(RZ, 4), [[-3, 4], [-16, 9]], ALU.is_ge, 0.0, -2, 1)
    sel(wr(RZ, 4), [[3, 4], [16, 9]], ALU.is_ge, 0.0, 3, -1)
    sel(wr(RC, 3), [[-3, 3], [-16, 9]], ALU.is_equal, 0.0, -4, 1)
    sel(wr(RG, 1), [[-16, 9]], ALU.not_equal, -16.0, -15, 1)
    sel(wr(RB, 2), [[0, 2], [-16, 9]], ALU.is_ge, 0.0, 0, 1)
    sel(wr(RB, 2), [[1, 2], [16, 9]], ALU.is_ge, 0.0, 14, -1)
    if "y" in OPT["mode"]:
        act(A("WR", MB * 144, MG * 144), A("SW", site(0, 0, 1), site(0, 0, 1) + 144), AF.Copy)
        iota(wr(RL, 1), [[0, 9]], 16, 0)
        sel(wr(RL, 1), [[-16, 9]], ALU.is_equal, 0.0, -15, 1)
    else:
        act(A("WR", MB * 144, NROLE * 144), A("WR", RB * 144, MB * 144), AF.Copy, scale=-0.5)
    iota(A("SEL", p=(0, 8)), [[0, 256]], 1, 0)
    sel(A("SEL", p=(0, 8)), [[0, 2], [-1, 8], [0, 16]], ALU.is_equal, 0.0, 0, 1)
    iota(A("DF"), [[0, 256]], 1, 0)
    sel(A("DF"), [[0, 2], [-1, 128]], ALU.is_equal, 0.0, 0, 1)
    iota(A("BO"), [[0, 128]], 1, 0)
    sel(A("BO"), [[-16, 8], [0, 16]], ALU.is_ge, 0.0, 0, 1)
    sel(A("BO"), [[16, 8], [0, 16]], ALU.is_ge, 0.0, 15, -1)
    iota(A("CJ"), [[16, HC]], 2 * H, 1)
    iota(A("CB"), [[16, HC]], 0, 0)
    for k in range(16):
        evac(A("MK", k * 128, (k + 1) * 128), A("BO"), col(LANE + k))
    late = block("SW", site(0, 1, 2))
    act(block("SW", site(0, 1, 1)), zero, AF.Copy)
    act(block("LW", _window(1, 0, 2)), zero, AF.Copy)
    for h in range(2):
        dma("y", block("SW", site(1, h, 1)), zero, late)
    dma("y", block("LW", _window(2, 0, 2)), zero, late)
    for j, sc in ((IDB, 1.0), (NEG, -1.0), (FLAG, -0.5 if "y" in OPT["mode"] else -256.0), (WIDE, float(H)), (BACK, -float(H)), (HIGH, 128.0),
                  (NTWO, -2.0), (TWO, 2.0)):
        n = 256 if j in (BACK, TWO, NTWO) else 128
        act(A("DB", j, j + n), A("DF", 0, n), AF.Copy, scale=sc)
    act(A("CJ"), A("CJ"), AF.Identity, bias=col(G16))
    ts(A("PLF", p=(0, 8)), A("PLI", p=(0, 8)), 2.0 ** -20, ALU.max)
    grp = []
    for t in range(STEPS):
        s = (-SH * (t + 1)) % 128
        bank, c0 = ("P0", t * C) if t < 2 else ("P1", 0)
        grp.append([(A(bank, c0, c0 + HC), A("SEL", 0, 128, p=(0, 8)), A("PLF", 0, HC, p=(0, 8)))])
        grp.append([(A(bank, c0 + HC, c0 + C), A("SEL", s, s + 128, p=(0, 8)), A("PLF", HC, C, p=(0, 8)))])
    mm(grp)
    evac(A("FS", 0, 2 * C), A("P0", 0, 2 * C))
    evac(A("FS", 2 * C, 3 * C), A("P1", 0, C))
    for t in range(STEPS):
        send(t + 1, A("FL", t * C, (t + 1) * C), A("FS", t * C, (t + 1) * C), "af%d" % t, True)

    def pb(h, j):
        return A("P%d" % (2 + 2 * h), j * HC, (j + 1) * HC)

    def pg(h, j):
        return A("P%d" % (3 + 2 * h), j * HC, (j + 1) * HC)

    def nh(t, h):
        return half("NH", h, (t % 2) * C)

    def names(t, h):
        return lists("LF", t, h) if t else half("NL", h)

    def aside(t, h):
        return OPT["mode"][2 * t + h] not in "gy"

    def dy(t, h):
        return ("DY", h * H) if aside(t, h) else ("SW", site(t, h, 0))

    def receptors(t, h):
        tag[0] = ("take", t, h)
        if t == 0:
            copy(lists("LU", 0, h), half("NL", h))
            if h:
                copy(lists("LF", 0, h), half("NL", h))
        else:
            copy(lists("LU", t, h, 0, 0, (h + 1) * HC), lists("LF", t, h, 0, 0, (h + 1) * HC))
            o, u = site(t, h, 2), _window(t, h, 2 * h)
            tag[0] = ("cells", t, h)
            for a, b in pieces(GQ):
                gather(A("SW", o + 16 * a, o + 16 * b), A("LW", u, u + 3 * H), lists("LU", t, h, 1, a, b))
        for j in (0,) * aside(t, h) + (-1,) * (t == STEPS - 1):
            dma("y", block("SW", site(t, h, j)), block("SW", site(t, h, 2)))
        if t < STEPS - 1:
            records(t, h, 0)

    def board(t, h):
        c = h * HC
        tag[0] = ("read", t, h)
        for a, b in pieces(GQ):
            gather(A("XG", 16 * (c + a), 16 * (c + b)), A("OW"), lists("LU", t, h, 0, a, b), col(MASKC + t), col(BIASC + t))
        tag[0] = ("mark", t, h)
        for a, b in pieces(SQ):
            mark(t, h, a, b)
        tag[0] = ("point", t, h)
        if t:
            extract(half("P6", h), RZ + t - 1, "XG", h * H)
            copy(half("PU", h), half("P6", h))
        if t < STEPS - 1:
            tag[0] = ("down", t, h)
            extract(half("P6", h, C), RD, "XG", h * H)
            copy(half("DU", h), half("P6", h, C))
            tt(half("DDF", h), half("P6", h, C), names(t, h), ALU.subtract)

    def mark(t, h, a, b):
        out, off, o = A("OW"), lists("LU", t, h, 0, a, b), h * H
        x, cc = A("XG", o + 16 * a, o + 16 * b), A("CC", o + 16 * a, o + 16 * b)
        add("v", "c", lambda q: g.vector.tensor_tensor(ind(out, off), x[0], cc[0], ALU.add), [x, cc, off], [out],
            US["v"] + x[2] * US["scatter"], sort="scatter")

    def differ(t, h, a, b):
        name, o = dy(t, h)
        out, win = A(name, o + 16 * a, o + 16 * b), A("BW", 0, W + t * K)
        off = A("PU", h * HC + a, h * HC + b) if t else lists("LU", 0, h, 0, a, b)
        r = A("SW", site(t, h, 2) + 16 * a, site(t, h, 2) + 16 * b)
        add("v", "c", lambda q: g.vector.tensor_tensor(out[0], ind(win, off), r[0], ALU.subtract), [win, off, r], [out],
            US["v"] + out[2] * US["gather"], sort="gather")
        ts(A("MM", mo(t, h) + 16 * a, mo(t, h) + 16 * b), out, A("EB", 0, 1), ALU.min, -2.0, ALU.mult)

    def least(out, win, off, r, y):
        if OPT["plain"]:
            return tt(out, y, r, ALU.min)
        add("v", "c", lambda q: g.vector.tensor_tensor(out[0], ind(win, off), r[0], ALU.min), [win, off, r], [out],
            US["v"] + out[2] * US["gather"], sort="gather")

    def links(t, h):
        if OPT["mode"][2 * t + h] == "y":
            win, o = A("BW", 0, W + t * K), site(t, h, 0)
            for a, b in pieces(GQ):
                off = A("PU", h * HC + a, h * HC + b) if t else lists("LU", 0, h, 0, a, b)
                tag[0] = ("visit", t, h)
                gather(A("SW", o + 16 * a, o + 16 * b), win, off)
                tag[0] = ("least", t, h)
                least(A("MM", mo(t, h) + 16 * a, mo(t, h) + 16 * b), win, off,
                      A("SW", site(t, h, 2) + 16 * a, site(t, h, 2) + 16 * b), A("SW", o + 16 * a, o + 16 * b))
            tag[0] = ("links", t, h)
            extract(pb(h, 0), RB, "MM", mo(t, h))
            extract(pg(h, 0), RG, "MM", mo(t, h))
            extract(pg(h, 3), RL, "SW", o)
            if t < STEPS - 1:
                records(t, h, 1)
            return
        for o, role in ((pb, RB), (pg, RG)):
            extract(o(h, 0), role, "SW", site(t, h, 2), last=False, bank=A(o(h, 0)[1][0]))
        for a, b in pieces(GQ):
            differ(t, h, a, b)
        for o, role in ((pb, MB), (pg, MG)):
            extract(o(h, 0), role, "MM", mo(t, h), first=False, bank=A(o(h, 0)[1][0]))
        if t < STEPS - 1 and OPT["fold"]:
            records(t, h, 1)
        accumulate(block("SW", site(t, h, 0)), block("DY", h * H) if aside(t, h) else block("SW", site(t, h, 2)))
        if t < STEPS - 1 and not OPT["fold"]:
            records(t, h, 1)

    def hold(t, h):
        tag[0] = ("hold", t, h)
        act(half("BD", h), pb(h, 0), AF.Sign)
        act(half("G1", h), pg(h, 0), AF.Relu, scale=1.0 - 2.0 ** -18)
        mm([[(pb(h, 1), A("BO"), half("BD", h))]])
        tt(half("WW", h), pb(h, 0), half("G1", h), ALU.subtract)
        tt(pb(h, 1), pb(h, 1), half("WW", h), ALU.mult)
        tt(nh(t, h), pb(h, 1), half("FL", h, t * C), ALU.is_lt)
        act(half("GT", h), half("G1", h), AF.Sign)
        if OPT["mode"][2 * t + h] == "y":
            return tt(half("EE", h), pg(h, 3), half("WW", h), ALU.is_gt)
        copy(half("RI", h), pg(h, 0))
        tt(half("EE", h), half("RI", h), pg(h, 0), ALU.subtract)

    def move(t, h):
        c = h * HC
        tag[0] = ("free", t, h)
        for a, b in pieces(GQ):
            gather(A("X4", 16 * (c + a), 16 * (c + b)), A("OW"), A("DU", c + a, c + b), empty=True)
        tag[0] = ("names", t, h)
        tt(half("UU", h), nh(t, h), half("DDF", h), ALU.mult)
        extract(half("P7", h), RC + t, "X4", h * H)
        tt(half("UU", h), half("P7", h), half("UU", h), ALU.mult)
        if not h:
            tt(lists("MO", t, 0), half("UU", 0), names(t, 0), ALU.add)
            send(1, lists("LF", t + 1, 0), lists("MO", t, 0), "an%d" % (t + 1), True)

    def swap(t, h):
        tag[0] = ("again", t, h)
        if not h:
            for a, b in pieces(GQ):
                gather(A("XC", 16 * a, 16 * b), A("OW"), lists("LU", t, 0, 0, a, b))
        tag[0] = ("list", t, h)
        o = pg(h, 1)
        extract(o, RC + t, "XG" if h else "XC", h * H,
                [(o, db(NEG), half("GT", h)), (o, db(FLAG), half("EE", h)), (o, db(NEG), nh(t, h))])
        act(half("VV", h), o, AF.Relu, bias=-1.0, scale=-2.0)
        o, iu = pg(h, 2), half("IU", h, t * C)
        mm([[(o, db(IDB), A("CB")), (o, db(WIDE), half("VV", h))]])
        ts(iu, o, col(KCOL), ALU.add)
        if t < STEPS - 1 and h:
            s, o, u = 128 - SH, half("P7", 0, C), half("P7", 1, C)
            mm([[(o, A("DF", s, s + 128), lists("LF", t, 1)), (o, A("DF", s, s + 128), half("UU", 1))],
                [(u, A("DF", 0, 128), A("CJ")), (u, db(BACK + s), half("VV", 1))]])
            evac(lists("MO", t, 1, 0, 0, C), A("P7", C, 2 * C))
            send(1, lists("LF", t + 1, 1, 0, 0, C), lists("MO", t, 1, 0, 0, C), "am%d" % (t + 1), True)
        elif t < STEPS - 1:
            send(1, lists("LU", t + 1, 0, 1), iu, "ai%d" % (t + 1), True)
        for name, u, j in ((("RS", h * H, -1),) if t == STEPS - 1 else ()) + (("BW", W + t * K + h * H, 0),):
            tag[0] = ("own" if j else "site", t, h)
            for a, b in pieces(GQ):
                gather(A(name, u + 16 * a, u + 16 * b), A("SW", site(t, h, j), site(t, h, j + 3)),
                       A("IU", t * C + h * HC + a, t * C + h * HC + b))

    def totals(t, h):
        s, x, e = (SH * (t + 1) * h) % 128, mo(t, h), h * H
        tail = 2 * t + h >= 2 * STEPS - OPT["tail"]
        acc = A("P6" if tail and h else "P7", 2 * C, 2 * C + HC)
        mode = OPT["mode"][2 * t + h]
        tag[0] = ("totals", t, h)
        terms = {"a": [], "y": [(IDB, "SW", site(t, h, 2)), (IDB, "SW", site(t, h, 0))], "d": [(IDB, "DY", h * H)], "g": [(NEG, "SW", site(t, h, 2)), (IDB, "SW", site(t, h, 0))]}[mode]
        if mode == "a":
            accumulate(block("MM", x), block("DY", h * H))
        for i in range(4):
            bank, grps = "P%d" % (i % 2), []
            for kk in range(4):
                k = 4 * i + kk
                o = A(bank, kk * HC, (kk + 1) * HC)
                grps.append([(o, db(NTWO if mode == "y" else IDB), A("MM", x + k, x + H, 16))]
                            + [(o, db(m), A(name, u + k, u + H, 16)) for m, name, u in terms]
                            + [(o, A("MK", k * 128, (k + 1) * 128), nh(t, h))])
            mm(grps)
            act(A("XE", e + i * 2 * C, e + (i + 1) * 2 * C), A(bank, 0, 2 * C), AF.Exp, scale=-1.0 / 64)
            if tail:
                mm([[(acc, A("DF", s, s + 128), half("XE", 0, e + k * HC)) for k in range(4 * i, 4 * i + 4)]],
                   i == 0, i == 3, A(acc[1][0]))
        if not tail:
            for n in (8 * HC, 4 * HC)[:OPT["halve"]]:
                accumulate(A("XE", e, e + n), A("XE", e + n, e + 2 * n))
            mm([[(acc, A("DF", s, s + 128), half("XE", 0, e + k * HC)) for k in range(16 >> OPT["halve"])]])
        evac(half("ES", h, t * C), acc)
        if h:
            send(-(t + 1), A("EL", t * C, (t + 1) * C), A("ES", t * C, (t + 1) * C), "ae%d" % t, True)

    def latest(t):
        tag[0] = ("latest", t, 0)
        for j in range(2):
            dma("y", A("DD", j * 256, (j + 1) * 256), A("OW", p=(2 + 3 * t + j, 128, 16)))
        o = A("P2", 256, 512)
        mm([[(o, db(IDB), A("DD", 0, 256)), (o, db(HIGH), A("DD", 256, 512))]])
        if t < STEPS - 1:
            evac(A("PF", 0, 256), o)
        else:
            tt(A("PF", 256, 512), o, A("PF", 0, 256), ALU.max)
            copy(A("PFU"), A("PF", 256, 512))

    for t in range(STEPS):
        for h in range(2):
            receptors(t, h)
            board(t, h)
            links(t, h)
            hold(t, h)
        tag[0] = None
        for j in range(2 if t < STEPS - 1 else 0):
            dma("y", A("CC", p=(2 + 3 * t + j, 128, 16)), A("SW", site(0, 0, 1), site(0, 0, 1) + 384, p=(0, 64)))
            if t:
                dma("y", A("CC", p=(5 + 3 * t + j, 128, 16)), A("JD", 384 * j, 384 * (j + 1), p=(0, 64)))
        for h in range(2):
            if t < STEPS - 1:
                move(t, h)
            swap(t, h)
        if t:
            latest(t)
        for h in range(2):
            totals(t, h)

    s = (SH * STEPS) % 128
    tag[0] = ("home", STEPS - 1, 0)
    for j in range(2):
        o, c = A("P%d" % (2 + j), 0, 384), j * 384
        mm([[(o, db(IDB), A("RS", c, c + 384)), (o, db(NEG), A("RS", c + 768, c + 768 + 384)),
             (o, db(TWO + s), A("RS", c + H, c + H + 384)), (o, db(NTWO + s), A("RS", c + H + 768, c + H + 768 + 384))]])
        evac(A("YS", j * 384, (j + 1) * 384), o)
        send(-STEPS, A("YL", j * 384, (j + 1) * 384), A("YS", j * 384, (j + 1) * 384), "ayr%d" % j, False)
        dma("y", T.yr[:, j * 384:(j + 1) * 384], A("YL", j * 384, (j + 1) * 384))
    tag[0] = ("wall", STEPS - 1, 0)
    for j in range(4):
        c = j * 1024
        gather(A("LW", c, c + 1024), A("BW"), A("PFU", j * 64, (j + 1) * 64))
        mm([[(A("P%d" % (4 + k // 2), (k % 2) * 256 + j * 64, (k % 2) * 256 + (j + 1) * 64), db(m),
              A("LW", c + 4 * u + k, c + 1024, 16)) for u, m in enumerate((IDB, NEG, TWO, NTWO))] for k in range(4)])
    for j in range(2):
        evac(A("YW", j * 512, (j + 1) * 512), A("P%d" % (4 + j)))
        dma("ys"[j], T.yw[:, j * 512:(j + 1) * 512], A("YW", j * 512, (j + 1) * 512))
    tag[0] = ("sum", STEPS - 1, 0)
    accumulate(A("EL", 0, C), A("EL", C, 2 * C))
    tt(A("EL", 3 * C, 4 * C), A("EL", 0, C), A("EL", 2 * C, 3 * C), ALU.add)
    dma("y", T.ye[:], A("EL", 3 * C, 4 * C))
    _emit(g, T, ops)
